import numpy as np
import ml_dtypes


def mxq(x, axis, fmt="e4m3"):
    dtype, down = {"e4m3": (ml_dtypes.float8_e4m3fn, 7), "e5m2": (ml_dtypes.float8_e5m2, 14)}[fmt]
    v = np.moveaxis(np.asarray(x, np.float32).astype(ml_dtypes.bfloat16).astype(np.float64), axis, -1)
    blocks = v.reshape(v.shape[:-1] + (-1, 32))
    amax = np.abs(blocks).max(-1, keepdims=True)
    byte = np.maximum(np.where(amax > 0, np.frexp(amax)[1] - 1 + 127, 0) - down, 1)
    scale = np.exp2(byte - 127.0)
    codes = (blocks / scale).astype(np.float32).astype(dtype).astype(np.float64)
    return np.moveaxis((codes * scale).reshape(v.shape), -1, axis)


WIDE = False


def mx_kscale(k):
    if not WIDE:
        return np.ones(k)
    levels = np.array([10, -10, 5, -5, 0])
    if k % 512:
        return np.exp2(np.random.permutation(np.resize(levels, k // 32))).repeat(32)
    a = np.empty((k // 512, 16))
    for p in range(k // 512):
        a[p, :8] = np.random.permutation(np.resize(levels, 8))
        for g in range(8):
            far = levels[np.abs(levels - a[p, g]) >= 10]
            a[p, g + 8] = far[np.random.randint(len(far))]
    return np.exp2(a.ravel()).repeat(32)


def f64(x):
    return np.asarray(x).astype(np.float64)


def striped(idx):
    return np.tile(np.asarray(idx).reshape(-1, 16).T, (8, 1)).astype(np.uint16)


def unstriped(offs):
    return offs[:16].T.reshape(-1).astype(np.int64)


E2M1 = np.array([0.0, 0.5, 1.0, 1.5, 2.0, 3.0, 4.0, 6.0, -0.0, -0.5, -1.0, -1.5, -2.0, -3.0, -4.0, -6.0])


def pack_weight(w, fmt):
    k, n = w.shape
    w = f64(np.asarray(w, np.float32).astype(ml_dtypes.bfloat16)).reshape(k // 32, 32, n)
    amax = np.abs(w).max(1)
    if fmt == "e4m3":
        byte = np.frexp(amax)[1] - 1 + 127 - 7
    else:
        mant, ex = np.frexp(amax / 6.0)
        byte = np.where(mant > 0.5, ex, ex - 1) + 127
    byte = np.clip(np.where(amax > 0, byte, 1), 1, 254)
    scaled = (w * np.exp2(127.0 - byte)[:, None, :]).reshape(k, n).astype(np.float32)
    by_word = np.ascontiguousarray(scaled.reshape(k // 512, 128, 4, n).transpose(0, 1, 3, 2))
    if fmt == "e4m3":
        words = by_word.astype(ml_dtypes.float8_e4m3fn).view(np.uint8)
    else:
        c = by_word.astype(ml_dtypes.float4_e2m1fn).view(np.uint8) & 0xF
        words = (c[..., 0::2] | (c[..., 1::2] << 4)).reshape(k // 512, 128, 2 * n)
    return np.ascontiguousarray(words), np.ascontiguousarray(byte.astype(np.uint8).reshape(k // 512, 16, n))


def unpack_weight(words, scales, fmt):
    g, _, n = scales.shape
    words = np.ascontiguousarray(words).reshape(g, 128, n, -1)
    if fmt == "e4m3":
        vals = words.view(ml_dtypes.float8_e4m3fn).astype(np.float64)
    else:
        nib = np.empty((g, 128, n, 4), np.uint8)
        nib[..., 0::2] = words & 0xF
        nib[..., 1::2] = words >> 4
        vals = E2M1[nib]
    vals = vals * np.repeat(np.exp2(scales.astype(np.float64) - 127.0), 8, axis=1)[..., None]
    return vals.transpose(0, 1, 3, 2).reshape(g * 512, n)


B, N, T, D, DV, NQ = 1, 1024, 4096, 512, 128, 128
PAGE = 512


def setup_inputs():
    n = np.random.standard_normal
    pages = np.random.permutation(T // PAGE)[:B * N // PAGE]
    idx = (pages[:, None] * PAGE + np.arange(PAGE)[None, :]).reshape(-1)
    s = mx_kscale(D)[:, None]
    u = np.ones(T)
    u[idx] = mx_kscale(B * N)
    r = np.random.uniform(0.5, 2.0, T)
    qp = [pack_weight(x, "e4m3") for x in n((B, D, NQ)) * s * (1.00 / np.sqrt(D))]
    k = n((D, T)) / s
    v = n((DV, T)) / (u * r)
    kp = pack_weight(k, "e4m3")
    vp = pack_weight(v.T, "e4m3")
    return {
        "q_words": np.stack([x[0] for x in qp]),
        "q_scales": np.stack([x[1] for x in qp]),
        "k_words": kp[0],
        "k_scales": kp[1],
        "v_words": vp[0],
        "v_scales": vp[1],
        "vs": np.tile(u * r, (128, 1)).astype(np.float32),
        "offs": striped(idx),
        "voffs": striped((pages[:, None] * DV + np.arange(DV)[None, :]).reshape(-1)),
    }


def reference(q_words, q_scales, k_words, k_scales, v_words, v_scales, vs, offs, voffs):
    idx = unstriped(offs)
    k = unpack_weight(k_words, k_scales, "e4m3")
    v = unpack_weight(v_words, v_scales, "e4m3")
    v = v.reshape(T // 512, 512, DV)[unstriped(voffs)[::DV] // DV].reshape(B, N, DV)
    pick = lambda x: x[:, idx].reshape(x.shape[0], B, N).transpose(1, 0, 2)
    q = np.stack([unpack_weight(q_words[b], q_scales[b], "e4m3") for b in range(B)])
    score = q.transpose(0, 2, 1) @ pick(k)
    p = score / (1.0 + np.exp(-score))
    w = p * pick(f64(vs))[:, :1, :]
    y = mxq(w, 2, "e4m3") @ v
    y = y / 16.0
    return y

@@ -1,0 +1,153 @@
+from contextlib import ExitStack
+
+import concourse.mybir as mybir
+from concourse.masks import make_identity
+
+P = 128
+T = 4096
+N = 1024
+PAGE = 512
+PAGES = N // PAGE
+POOL_PAGES = T // PAGE
+NQ = 128
+DV = 128
+D = 512
+PACK = 4
+HALF = NQ // 2
+VS_ROW = P - 1
+Q_SHIFT = 4
+V_SHIFT = 8
+
+FLOPS = 2 * NQ * N * D + 2 * NQ * N * DV
+
+F32 = mybir.dt.float32
+BF16 = mybir.dt.bfloat16
+I32 = mybir.dt.int32
+U32 = mybir.dt.uint32
+U16 = mybir.dt.uint16
+U8 = mybir.dt.uint8
+FP8X4 = mybir.dt.float8_e4m3fn_x4
+MULT = mybir.AluOpType.mult
+SILU = mybir.ActivationFunctionType.Silu
+COPY = mybir.ActivationFunctionType.Copy
+
+
+def tile_attend_pkv8q_silu_kernel(
+    tc, q_words, q_scales, k_words, k_scales, v_words, v_scales, vs, offs, voffs, out
+):
+    nc = tc.nc
+    with ExitStack() as ctx:
+        sb = ctx.enter_context(tc.tile_pool(name="sb", bufs=1))
+        ps = ctx.enter_context(tc.psum_pool(name="ps", bufs=1))
+
+        offs_t = sb.tile([P, N // 16], U16, name="offs_t")
+        voffs_t = sb.tile([P, PAGES * DV // 16], U16, name="voffs_t")
+        kw_pool = sb.tile([P, T], I32, name="kw_pool", align_bytes=64)
+        ks_pool = sb.tile([P, T], U8, name="ks_pool", align_bytes=64)
+        vw_pool = sb.tile([P, POOL_PAGES * DV], I32, name="vw_pool", align_bytes=64)
+        vsc_pool = sb.tile([P, POOL_PAGES * DV], U8, name="vsc_pool", align_bytes=64)
+        vs_pool = sb.tile([P, T], F32, name="vs_pool", align_bytes=64)
+        qw = sb.tile([P, NQ], I32, name="qw", align_bytes=64)
+        qs = sb.tile([P, NQ], U8, name="qs", align_bytes=64)
+        ident = sb.tile([P, P], F32, name="ident", align_bytes=64)
+
+        nc.vector.memset(qs[:].bitcast(I32), 0)
+        nc.vector.memset(ks_pool[:].bitcast(I32), 0)
+        nc.vector.memset(vs_pool[0:VS_ROW, :], 0.0)
+        make_identity(nc, ident[:])
+        nc.gpsimd.memset(vsc_pool[:].bitcast(I32), 0)
+
+        def load_qs(eng, quad):
+            r = 32 * quad + Q_SHIFT
+            eng.dma_start(qs[r : r + 4, :].bitcast(I32), q_scales[0, 0, 4 * quad : 4 * quad + 4, :].bitcast(I32))
+
+        nc.sync.dma_start(offs_t[:], offs)
+        nc.scalar.dma_start(vs_pool[VS_ROW:P, :], vs[0:1, :])
+        nc.sync.dma_start(voffs_t[:], voffs)
+        nc.scalar.dma_start(qw[:], q_words[0, 0].rearrange("p n t -> p (n t)").bitcast(I32))
+        load_qs(nc.sync, 0)
+        load_qs(nc.scalar, 1)
+        nc.sync.dma_start(kw_pool[:], k_words[0].rearrange("p n t -> p (n t)").bitcast(I32))
+        nc.sync.dma_start(
+            vw_pool[:].rearrange("p (u e) -> p u e", u=POOL_PAGES),
+            v_words.rearrange("u p e t -> p u (e t)").bitcast(I32),
+        )
+        for quad in range(4):
+            nc.scalar.dma_start(
+                ks_pool[32 * quad : 32 * quad + 4, :].bitcast(I32),
+                k_scales[0, 4 * quad : 4 * quad + 4, :].bitcast(I32),
+            )
+        load_qs(nc.scalar, 2)
+        load_qs(nc.scalar, 3)
+        for quad in range(4):
+            r = 32 * quad + V_SHIFT
+            nc.gpsimd.dma_start(
+                vsc_pool[r : r + 4, :].bitcast(I32).rearrange("r (u e) -> r u e", u=POOL_PAGES),
+                v_scales[:, 4 * quad : 4 * quad + 4, :].bitcast(I32).rearrange("u r e -> r u e"),
+            )
+
+        vs_g = sb.tile([P, N], F32, name="vs_g", align_bytes=64)
+        nc.vector.tensor_copy(vs_g[:], vs_pool[:].indirect(offs_t[:]))
+        vs_t = [ps.tile([P, PACK, P], F32, name=f"vs_t{g}") for g in range(PAGES)]
+        for g in range(PAGES):
+            for t in range(PACK):
+                nc.tensor.transpose(vs_t[g][:, t, :], vs_g[:, g * PAGE + t : (g + 1) * PAGE : PACK], ident[:])
+
+        ks_g = sb.tile([P, N], U8, name="ks_g", align_bytes=64)
+        ks_p = sb.tile([P, N], U8, name="ks_p", align_bytes=64)
+        nc.vector.tensor_copy(ks_g[:], ks_pool[:].indirect(offs_t[:]))
+        nc.vector.tensor_copy(
+            ks_p[:].rearrange("p (g t s) -> p g t s", g=PAGES, t=PACK),
+            ks_g[:].rearrange("p (g s t) -> p g t s", g=PAGES, t=PACK),
+        )
+
+        kw_g = [sb.tile([P, PAGE], U32, name=f"kw_g{g}", align_bytes=64) for g in range(PAGES)]
+        score = [ps.tile([P, PACK, NQ], F32, name=f"score{g}") for g in range(PAGES)]
+        for g in range(PAGES):
+            nc.vector.tensor_copy(
+                kw_g[g][:].rearrange("p (t s) -> p s t", t=PACK),
+                kw_pool[:].bitcast(U32).indirect(offs_t[:, g * (PAGE // 16) : (g + 1) * (PAGE // 16)]),
+            )
+            for t in range(PACK):
+                nc.tensor.matmul_mx(
+                    out=score[g][:, t, :],
+                    lhsT=kw_g[g][:, t * P : (t + 1) * P].bitcast(FP8X4),
+                    lhsT_scale=ks_p[:, g * PAGE + t * P : g * PAGE + (t + 1) * P],
+                    rhs=qw[:].bitcast(FP8X4),
+                    rhs_scale=qs[Q_SHIFT:P, :],
+                    start=True,
+                    stop=True,
+                )
+        vsc_g = sb.tile([P, PAGES * DV], U8, name="vsc_g", align_bytes=64)
+        nc.vector.tensor_copy(vsc_g[:], vsc_pool[:].indirect(voffs_t[:]))
+        vw_g = sb.tile([P, PAGES * DV], U32, name="vw_g", align_bytes=64)
+        nc.vector.tensor_copy(vw_g[:], vw_pool[:].bitcast(U32).indirect(voffs_t[:]))
+
+        acc = ps.tile([P, DV], F32, name="acc")
+        for g in range(PAGES):
+            w16 = sb.tile([P, NQ, PACK], BF16, name=f"w16_{g}", align_bytes=64)
+            for h in range(2):
+                cols = slice(h * HALF, (h + 1) * HALF)
+                p32 = sb.tile([P, HALF, PACK], F32, name=f"p32_{g}{h}", align_bytes=64)
+                nc.scalar.activation(p32[:], score[g][:, :, cols].rearrange("p t q -> p q t"), SILU)
+                nc.vector.tensor_tensor(
+                    w16[:, cols, :],
+                    p32[:],
+                    vs_t[g][:, :, VS_ROW:P].rearrange("p t o -> p o t").to_broadcast([P, HALF, PACK]),
+                    MULT,
+                )
+            wq = sb.tile([P, NQ], U32, name=f"wq{g}", align_bytes=64)
+            wsc = sb.tile([P, NQ], U8, name=f"wsc{g}", align_bytes=64)
+            nc.vector.quantize_mx(out=wq[:].bitcast(FP8X4), scales=wsc[:], in_=w16[:].rearrange("p q t -> p (q t)"))
+            nc.tensor.matmul_mx(
+                out=acc[:],
+                lhsT=wq[:].bitcast(FP8X4),
+                lhsT_scale=wsc[:],
+                rhs=vw_g[:, g * DV : (g + 1) * DV].bitcast(FP8X4),
+                rhs_scale=vsc_g[V_SHIFT:P, g * DV : (g + 1) * DV],
+                start=(g == 0),
+                stop=(g == PAGES - 1),
+            )
+        y = sb.tile([P, DV], F32, name="y", align_bytes=64)
+        nc.scalar.activation(y[:], acc[:], COPY, scale=1.0 / 16.0)
+        nc.sync.dma_start(out[0], y[:])

@@ -42,7 +42,7 @@ def tile_attend_pkv8q_silu_kernel(
 
         offs_t = sb.tile([P, N // 16], U16, name="offs_t")
         voffs_t = sb.tile([P, PAGES * DV // 16], U16, name="voffs_t")
-        kw_pool = sb.tile([P, T], I32, name="kw_pool", align_bytes=64)
+        kw_pool = sb.tile([P, T], I32, name="kw_pool", tag="kw_pool", align_bytes=64)
         ks_pool = sb.tile([P, T], U8, name="ks_pool", align_bytes=64)
         vw_pool = sb.tile([P, POOL_PAGES * DV], I32, name="vw_pool", align_bytes=64)
         vsc_pool = sb.tile([P, POOL_PAGES * DV], U8, name="vsc_pool", align_bytes=64)
@@ -51,49 +51,40 @@ def tile_attend_pkv8q_silu_kernel(
         qs = sb.tile([P, NQ], U8, name="qs", align_bytes=64)
         ident = sb.tile([P, P], F32, name="ident", align_bytes=64)
 
-        nc.vector.memset(qs[:].bitcast(I32), 0)
-        nc.vector.memset(ks_pool[:].bitcast(I32), 0)
-        nc.vector.memset(vs_pool[0:VS_ROW, :], 0.0)
+        nc.gpsimd.memset(qs[:].bitcast(I32), 0)
         make_identity(nc, ident[:])
-        nc.gpsimd.memset(vsc_pool[:].bitcast(I32), 0)
-
-        def load_qs(eng, quad):
-            r = 32 * quad + Q_SHIFT
-            eng.dma_start(qs[r : r + 4, :].bitcast(I32), q_scales[0, 0, 4 * quad : 4 * quad + 4, :].bitcast(I32))
+        nc.gpsimd.memset(ks_pool[:].bitcast(I32), 0)
+        vs_zero = vs_pool[0:VS_ROW, :].bitcast(I32)
+        nc.vector.memset(vs_zero[:, 0:1791], 0)
+        nc.vector.memset(vs_zero[:, 1791:1792], 0)
+        nc.vector.memset(vs_zero[:, 1792:T], 0)
 
         nc.sync.dma_start(offs_t[:], offs)
-        nc.scalar.dma_start(vs_pool[VS_ROW:P, :], vs[0:1, :])
+        nc.sync.dma_start(vs_pool[VS_ROW:P, :], vs[0:1, :])
         nc.sync.dma_start(voffs_t[:], voffs)
-        nc.scalar.dma_start(qw[:], q_words[0, 0].rearrange("p n t -> p (n t)").bitcast(I32))
-        load_qs(nc.sync, 0)
-        load_qs(nc.scalar, 1)
+        for quad in range(4):
+            r = 32 * quad + Q_SHIFT
+            nc.scalar.dma_start(qs[r : r + 4, :].bitcast(I32), q_scales[0, 0, 4 * quad : 4 * quad + 4, :].bitcast(I32))
         nc.sync.dma_start(kw_pool[:], k_words[0].rearrange("p n t -> p (n t)").bitcast(I32))
+        nc.sync.dma_start(qw[:], q_words[0, 0].rearrange("p n t -> p (n t)").bitcast(I32))
         nc.sync.dma_start(
             vw_pool[:].rearrange("p (u e) -> p u e", u=POOL_PAGES),
             v_words.rearrange("u p e t -> p u (e t)").bitcast(I32),
         )
-        for quad in range(4):
+        for quad in (0, 2, 1, 3):
             nc.scalar.dma_start(
                 ks_pool[32 * quad : 32 * quad + 4, :].bitcast(I32),
                 k_scales[0, 4 * quad : 4 * quad + 4, :].bitcast(I32),
             )
-        load_qs(nc.scalar, 2)
-        load_qs(nc.scalar, 3)
-        for quad in range(4):
-            r = 32 * quad + V_SHIFT
-            nc.gpsimd.dma_start(
-                vsc_pool[r : r + 4, :].bitcast(I32).rearrange("r (u e) -> r u e", u=POOL_PAGES),
-                v_scales[:, 4 * quad : 4 * quad + 4, :].bitcast(I32).rearrange("u r e -> r u e"),
-            )
 
         vs_g = sb.tile([P, N], F32, name="vs_g", align_bytes=64)
         nc.vector.tensor_copy(vs_g[:], vs_pool[:].indirect(offs_t[:]))
-        vs_t = [ps.tile([P, PACK, P], F32, name=f"vs_t{g}") for g in range(PAGES)]
-        for g in range(PAGES):
-            for t in range(PACK):
-                nc.tensor.transpose(vs_t[g][:, t, :], vs_g[:, g * PAGE + t : (g + 1) * PAGE : PACK], ident[:])
+        vs_t = ps.tile([P, 2 * P], F32, name="vs_t")
+        for j in reversed(range(PAGES * PACK)):
+            g, t = divmod(j, PACK)
+            nc.tensor.transpose(vs_t[:, j + 1 : j + 1 + P], vs_g[:, g * PAGE + t : (g + 1) * PAGE : PACK], ident[:])
 
-        ks_g = sb.tile([P, N], U8, name="ks_g", align_bytes=64)
+        ks_g = sb.tile([P, N], U8, name="ks_g", tag="kw_g", align_bytes=64)
         ks_p = sb.tile([P, N], U8, name="ks_p", align_bytes=64)
         nc.vector.tensor_copy(ks_g[:], ks_pool[:].indirect(offs_t[:]))
         nc.vector.tensor_copy(
@@ -101,48 +92,70 @@ def tile_attend_pkv8q_silu_kernel(
             ks_g[:].rearrange("p (g s t) -> p g t s", g=PAGES, t=PACK),
         )
 
-        kw_g = [sb.tile([P, PAGE], U32, name=f"kw_g{g}", align_bytes=64) for g in range(PAGES)]
+        nc.vector.memset(vsc_pool[:].bitcast(I32), 0)
+        for quad in range(4):
+            r = 32 * quad + V_SHIFT
+            nc.sync.dma_start(
+                vsc_pool[r : r + 4, :].bitcast(I32).rearrange("r (u e) -> r u e", u=POOL_PAGES),
+                v_scales[:, 4 * quad : 4 * quad + 4, :].bitcast(I32).rearrange("u r e -> r u e"),
+            )
+
+        kw_g = sb.tile([P, N], U32, name="kw_g", tag="kw_g", align_bytes=64)
         score = [ps.tile([P, PACK, NQ], F32, name=f"score{g}") for g in range(PAGES)]
         for g in range(PAGES):
             nc.vector.tensor_copy(
-                kw_g[g][:].rearrange("p (t s) -> p s t", t=PACK),
+                kw_g[:, g * PAGE : (g + 1) * PAGE].rearrange("p (t s) -> p s t", t=PACK),
                 kw_pool[:].bitcast(U32).indirect(offs_t[:, g * (PAGE // 16) : (g + 1) * (PAGE // 16)]),
             )
             for t in range(PACK):
+                slots = slice(g * PAGE + t * P, g * PAGE + (t + 1) * P)
                 nc.tensor.matmul_mx(
                     out=score[g][:, t, :],
-                    lhsT=kw_g[g][:, t * P : (t + 1) * P].bitcast(FP8X4),
-                    lhsT_scale=ks_p[:, g * PAGE + t * P : g * PAGE + (t + 1) * P],
+                    lhsT=kw_g[:, slots].bitcast(FP8X4),
+                    lhsT_scale=ks_p[:, slots],
                     rhs=qw[:].bitcast(FP8X4),
                     rhs_scale=qs[Q_SHIFT:P, :],
                     start=True,
                     stop=True,
                 )
-        vsc_g = sb.tile([P, PAGES * DV], U8, name="vsc_g", align_bytes=64)
-        nc.vector.tensor_copy(vsc_g[:], vsc_pool[:].indirect(voffs_t[:]))
-        vw_g = sb.tile([P, PAGES * DV], U32, name="vw_g", align_bytes=64)
+        vw_g = sb.tile([P, PAGES * DV], U32, name="vw_g", tag="kw_pool", align_bytes=64)
         nc.vector.tensor_copy(vw_g[:], vw_pool[:].bitcast(U32).indirect(voffs_t[:]))
+
+        w16 = [sb.tile([P, NQ, PACK], BF16, name=f"w16_{g}", align_bytes=64) for g in range(PAGES)]
+        wq = [sb.tile([P, NQ], U32, name=f"wq{g}", align_bytes=64) for g in range(PAGES)]
+        wsc = [sb.tile([P, NQ], U8, name=f"wsc{g}", align_bytes=64) for g in range(PAGES)]
+
+        def weigh(g, h):
+            cols = slice(h * HALF, (h + 1) * HALF)
+            p32 = sb.tile([P, HALF, PACK], F32, name=f"p32_{g}{h}", tag=f"p32_{g}{h}", align_bytes=64)
+            nc.scalar.activation(p32[:], score[g][:, :, cols].rearrange("p t q -> p q t"), SILU)
+            nc.vector.tensor_tensor(
+                w16[g][:, cols, :],
+                p32[:],
+                vs_t[:, P + g * PACK : P + (g + 1) * PACK].unsqueeze(1).to_broadcast([P, HALF, PACK]),
+                MULT,
+            )
+
+        def quantize(g):
+            nc.vector.quantize_mx(
+                out=wq[g][:].bitcast(FP8X4), scales=wsc[g][:], in_=w16[g][:].rearrange("p q t -> p (q t)")
+            )
+
+        weigh(0, 0)
+        weigh(0, 1)
+        weigh(1, 0)
+        quantize(0)
+        weigh(1, 1)
+        vsc_g = sb.tile([P, PAGES * DV], U8, name="vsc_g", tag="p32_11", align_bytes=64)
+        nc.vector.tensor_copy(vsc_g[:], vsc_pool[:].indirect(voffs_t[:]))
+        quantize(1)
 
         acc = ps.tile([P, DV], F32, name="acc")
         for g in range(PAGES):
-            w16 = sb.tile([P, NQ, PACK], BF16, name=f"w16_{g}", align_bytes=64)
-            for h in range(2):
-                cols = slice(h * HALF, (h + 1) * HALF)
-                p32 = sb.tile([P, HALF, PACK], F32, name=f"p32_{g}{h}", align_bytes=64)
-                nc.scalar.activation(p32[:], score[g][:, :, cols].rearrange("p t q -> p q t"), SILU)
-                nc.vector.tensor_tensor(
-                    w16[:, cols, :],
-                    p32[:],
-                    vs_t[g][:, :, VS_ROW:P].rearrange("p t o -> p o t").to_broadcast([P, HALF, PACK]),
-                    MULT,
-                )
-            wq = sb.tile([P, NQ], U32, name=f"wq{g}", align_bytes=64)
-            wsc = sb.tile([P, NQ], U8, name=f"wsc{g}", align_bytes=64)
-            nc.vector.quantize_mx(out=wq[:].bitcast(FP8X4), scales=wsc[:], in_=w16[:].rearrange("p q t -> p (q t)"))
             nc.tensor.matmul_mx(
                 out=acc[:],
-                lhsT=wq[:].bitcast(FP8X4),
-                lhsT_scale=wsc[:],
+                lhsT=wq[g][:].bitcast(FP8X4),
+                lhsT_scale=wsc[g][:],
                 rhs=vw_g[:, g * DV : (g + 1) * DV].bitcast(FP8X4),
                 rhs_scale=vsc_g[V_SHIFT:P, g * DV : (g + 1) * DV],
                 start=(g == 0),

@@ -44,38 +44,36 @@ def tile_attend_pkv8q_silu_kernel(
         voffs_t = sb.tile([P, PAGES * DV // 16], U16, name="voffs_t")
         kw_pool = sb.tile([P, T], I32, name="kw_pool", tag="kw_pool", align_bytes=64)
         ks_pool = sb.tile([P, T], U8, name="ks_pool", align_bytes=64)
-        vw_pool = sb.tile([P, POOL_PAGES * DV], I32, name="vw_pool", align_bytes=64)
-        vsc_pool = sb.tile([P, POOL_PAGES * DV], U8, name="vsc_pool", align_bytes=64)
-        vs_pool = sb.tile([P, T], F32, name="vs_pool", align_bytes=64)
+        vs_pool = sb.tile([P, T], F32, name="vs_pool", tag="vs_pool", align_bytes=64)
         qw = sb.tile([P, NQ], I32, name="qw", align_bytes=64)
         qs = sb.tile([P, NQ], U8, name="qs", align_bytes=64)
         ident = sb.tile([P, P], F32, name="ident", align_bytes=64)
 
-        nc.gpsimd.memset(qs[:].bitcast(I32), 0)
-        make_identity(nc, ident[:])
-        nc.gpsimd.memset(ks_pool[:].bitcast(I32), 0)
-        vs_zero = vs_pool[0:VS_ROW, :].bitcast(I32)
-        nc.vector.memset(vs_zero[:, 0:1791], 0)
-        nc.vector.memset(vs_zero[:, 1791:1792], 0)
-        nc.vector.memset(vs_zero[:, 1792:T], 0)
+        nc.vector.memset(ks_pool[:].bitcast(I32), 0)
+        nc.vector.memset(qs[:].bitcast(I32), 0)
+        nc.vector.memset(vs_pool[0:VS_ROW, :].bitcast(I32), 0)
+        nc.vector.memset(ident[:], 0.0)
+        make_identity(nc, ident[:], nomemset=True)
 
         nc.sync.dma_start(offs_t[:], offs)
         nc.sync.dma_start(vs_pool[VS_ROW:P, :], vs[0:1, :])
         nc.sync.dma_start(voffs_t[:], voffs)
-        for quad in range(4):
-            r = 32 * quad + Q_SHIFT
-            nc.scalar.dma_start(qs[r : r + 4, :].bitcast(I32), q_scales[0, 0, 4 * quad : 4 * quad + 4, :].bitcast(I32))
+        for quad in (0, 2, 1, 3):
+            nc.sync.dma_start(
+                ks_pool[32 * quad : 32 * quad + 4, :].bitcast(I32),
+                k_scales[0, 4 * quad : 4 * quad + 4, :].bitcast(I32),
+            )
         nc.sync.dma_start(kw_pool[:], k_words[0].rearrange("p n t -> p (n t)").bitcast(I32))
         nc.sync.dma_start(qw[:], q_words[0, 0].rearrange("p n t -> p (n t)").bitcast(I32))
+        for quad in range(4):
+            r = 32 * quad + Q_SHIFT
+            nc.sync.dma_start(qs[r : r + 4, :].bitcast(I32), q_scales[0, 0, 4 * quad : 4 * quad + 4, :].bitcast(I32))
+
+        vw_pool = sb.tile([P, POOL_PAGES * DV], I32, name="vw_pool", align_bytes=64)
         nc.sync.dma_start(
             vw_pool[:].rearrange("p (u e) -> p u e", u=POOL_PAGES),
             v_words.rearrange("u p e t -> p u (e t)").bitcast(I32),
         )
-        for quad in (0, 2, 1, 3):
-            nc.scalar.dma_start(
-                ks_pool[32 * quad : 32 * quad + 4, :].bitcast(I32),
-                k_scales[0, 4 * quad : 4 * quad + 4, :].bitcast(I32),
-            )
 
         vs_g = sb.tile([P, N], F32, name="vs_g", align_bytes=64)
         nc.vector.tensor_copy(vs_g[:], vs_pool[:].indirect(offs_t[:]))
@@ -84,15 +82,8 @@ def tile_attend_pkv8q_silu_kernel(
             g, t = divmod(j, PACK)
             nc.tensor.transpose(vs_t[:, j + 1 : j + 1 + P], vs_g[:, g * PAGE + t : (g + 1) * PAGE : PACK], ident[:])
 
-        ks_g = sb.tile([P, N], U8, name="ks_g", tag="kw_g", align_bytes=64)
-        ks_p = sb.tile([P, N], U8, name="ks_p", align_bytes=64)
-        nc.vector.tensor_copy(ks_g[:], ks_pool[:].indirect(offs_t[:]))
-        nc.vector.tensor_copy(
-            ks_p[:].rearrange("p (g t s) -> p g t s", g=PAGES, t=PACK),
-            ks_g[:].rearrange("p (g s t) -> p g t s", g=PAGES, t=PACK),
-        )
-
-        nc.vector.memset(vsc_pool[:].bitcast(I32), 0)
+        vsc_pool = sb.tile([P, POOL_PAGES * DV], U8, name="vsc_pool", tag="vs_pool", align_bytes=64)
+        nc.gpsimd.memset(vsc_pool[:].bitcast(I32), 0)
         for quad in range(4):
             r = 32 * quad + V_SHIFT
             nc.sync.dma_start(
@@ -100,6 +91,13 @@ def tile_attend_pkv8q_silu_kernel(
                 v_scales[:, 4 * quad : 4 * quad + 4, :].bitcast(I32).rearrange("u r e -> r u e"),
             )
 
+        ks_g = sb.tile([P, N], U8, name="ks_g", tag="kw_g", align_bytes=64)
+        ks_p = sb.tile([P, N], U8, name="ks_p", align_bytes=64)
+        nc.vector.tensor_copy(ks_g[:], ks_pool[:].indirect(offs_t[:]))
+        nc.vector.tensor_copy(
+            ks_p[:].rearrange("p (g t s) -> p g t s", g=PAGES, t=PACK),
+            ks_g[:].rearrange("p (g s t) -> p g t s", g=PAGES, t=PACK),
+        )
         kw_g = sb.tile([P, N], U32, name="kw_g", tag="kw_g", align_bytes=64)
         score = [ps.tile([P, PACK, NQ], F32, name=f"score{g}") for g in range(PAGES)]
         for g in range(PAGES):

@@ -17,6 +17,7 @@ HALF = NQ // 2
 VS_ROW = P - 1
 Q_SHIFT = 4
 V_SHIFT = 8
+HEAD = 512
 
 FLOPS = 2 * NQ * N * D + 2 * NQ * N * DV
 
@@ -42,9 +43,9 @@ def tile_attend_pkv8q_silu_kernel(
 
         offs_t = sb.tile([P, N // 16], U16, name="offs_t")
         voffs_t = sb.tile([P, PAGES * DV // 16], U16, name="voffs_t")
-        kw_pool = sb.tile([P, T], I32, name="kw_pool", tag="kw_pool", align_bytes=64)
+        kw_pool = sb.tile([P, T], I32, name="kw_pool", align_bytes=64)
         ks_pool = sb.tile([P, T], U8, name="ks_pool", align_bytes=64)
-        vs_pool = sb.tile([P, T], F32, name="vs_pool", tag="vs_pool", align_bytes=64)
+        vs_pool = sb.tile([P, T], F32, name="vs_pool", align_bytes=64)
         qw = sb.tile([P, NQ], I32, name="qw", align_bytes=64)
         qs = sb.tile([P, NQ], U8, name="qs", align_bytes=64)
         ident = sb.tile([P, P], F32, name="ident", align_bytes=64)
@@ -55,7 +56,9 @@ def tile_attend_pkv8q_silu_kernel(
         nc.vector.memset(ident[:], 0.0)
         make_identity(nc, ident[:], nomemset=True)
 
+        kw_hbm = k_words[0].rearrange("p n t -> p (n t)").bitcast(I32)
         nc.sync.dma_start(offs_t[:], offs)
+        nc.sync.dma_start(kw_pool[:, 0:HEAD], kw_hbm[:, 0:HEAD])
         nc.sync.dma_start(vs_pool[VS_ROW:P, :], vs[0:1, :])
         nc.sync.dma_start(voffs_t[:], voffs)
         for quad in (0, 2, 1, 3):
@@ -63,7 +66,7 @@ def tile_attend_pkv8q_silu_kernel(
                 ks_pool[32 * quad : 32 * quad + 4, :].bitcast(I32),
                 k_scales[0, 4 * quad : 4 * quad + 4, :].bitcast(I32),
             )
-        nc.sync.dma_start(kw_pool[:], k_words[0].rearrange("p n t -> p (n t)").bitcast(I32))
+        nc.sync.dma_start(kw_pool[:, HEAD:T], kw_hbm[:, HEAD:T])
         nc.sync.dma_start(qw[:], q_words[0, 0].rearrange("p n t -> p (n t)").bitcast(I32))
         for quad in range(4):
             r = 32 * quad + Q_SHIFT
@@ -82,8 +85,11 @@ def tile_attend_pkv8q_silu_kernel(
             g, t = divmod(j, PACK)
             nc.tensor.transpose(vs_t[:, j + 1 : j + 1 + P], vs_g[:, g * PAGE + t : (g + 1) * PAGE : PACK], ident[:])
 
-        vsc_pool = sb.tile([P, POOL_PAGES * DV], U8, name="vsc_pool", tag="vs_pool", align_bytes=64)
-        nc.gpsimd.memset(vsc_pool[:].bitcast(I32), 0)
+        ks_g = sb.tile([P, N], U8, name="ks_g", align_bytes=64)
+        ks_p = sb.tile([P, N], U8, name="ks_p", align_bytes=64)
+        nc.vector.tensor_copy(ks_g[:], ks_pool[:].indirect(offs_t[:]))
+        vsc_pool = sb.tile([P, POOL_PAGES * DV], U8, name="vsc_pool", align_bytes=64)
+        nc.vector.memset(vsc_pool[:].bitcast(I32), 0)
         for quad in range(4):
             r = 32 * quad + V_SHIFT
             nc.sync.dma_start(
@@ -91,14 +97,11 @@ def tile_attend_pkv8q_silu_kernel(
                 v_scales[:, 4 * quad : 4 * quad + 4, :].bitcast(I32).rearrange("u r e -> r u e"),
             )
 
-        ks_g = sb.tile([P, N], U8, name="ks_g", tag="kw_g", align_bytes=64)
-        ks_p = sb.tile([P, N], U8, name="ks_p", align_bytes=64)
-        nc.vector.tensor_copy(ks_g[:], ks_pool[:].indirect(offs_t[:]))
         nc.vector.tensor_copy(
             ks_p[:].rearrange("p (g t s) -> p g t s", g=PAGES, t=PACK),
             ks_g[:].rearrange("p (g s t) -> p g t s", g=PAGES, t=PACK),
         )
-        kw_g = sb.tile([P, N], U32, name="kw_g", tag="kw_g", align_bytes=64)
+        kw_g = sb.tile([P, N], U32, name="kw_g", align_bytes=64)
         score = [ps.tile([P, PACK, NQ], F32, name=f"score{g}") for g in range(PAGES)]
         for g in range(PAGES):
             nc.vector.tensor_copy(
@@ -116,7 +119,7 @@ def tile_attend_pkv8q_silu_kernel(
                     start=True,
                     stop=True,
                 )
-        vw_g = sb.tile([P, PAGES * DV], U32, name="vw_g", tag="kw_pool", align_bytes=64)
+        vw_g = sb.tile([P, PAGES * DV], U32, name="vw_g", align_bytes=64)
         nc.vector.tensor_copy(vw_g[:], vw_pool[:].bitcast(U32).indirect(voffs_t[:]))
 
         w16 = [sb.tile([P, NQ, PACK], BF16, name=f"w16_{g}", align_bytes=64) for g in range(PAGES)]
@@ -144,7 +147,7 @@ def tile_attend_pkv8q_silu_kernel(
         weigh(1, 0)
         quantize(0)
         weigh(1, 1)
-        vsc_g = sb.tile([P, PAGES * DV], U8, name="vsc_g", tag="p32_11", align_bytes=64)
+        vsc_g = sb.tile([P, PAGES * DV], U8, name="vsc_g", tag="p32_10", align_bytes=64)
         nc.vector.tensor_copy(vsc_g[:], vsc_pool[:].indirect(voffs_t[:]))
         quantize(1)
 

@@ -51,10 +51,11 @@ def tile_attend_pkv8q_silu_kernel(
         ident = sb.tile([P, P], F32, name="ident", align_bytes=64)
 
         nc.vector.memset(ks_pool[:].bitcast(I32), 0)
-        nc.vector.memset(qs[:].bitcast(I32), 0)
         nc.vector.memset(vs_pool[0:VS_ROW, :].bitcast(I32), 0)
-        nc.vector.memset(ident[:], 0.0)
-        make_identity(nc, ident[:], nomemset=True)
+        nc.gpsimd.memset(qs[:].bitcast(I32), 0)
+        vsc_pool = sb.tile([P, POOL_PAGES * DV], U8, name="vsc_pool", align_bytes=64)
+        nc.gpsimd.memset(vsc_pool[:].bitcast(I32), 0)
+        make_identity(nc, ident[:])
 
         kw_hbm = k_words[0].rearrange("p n t -> p (n t)").bitcast(I32)
         nc.sync.dma_start(offs_t[:], offs)
@@ -88,8 +89,6 @@ def tile_attend_pkv8q_silu_kernel(
         ks_g = sb.tile([P, N], U8, name="ks_g", align_bytes=64)
         ks_p = sb.tile([P, N], U8, name="ks_p", align_bytes=64)
         nc.vector.tensor_copy(ks_g[:], ks_pool[:].indirect(offs_t[:]))
-        vsc_pool = sb.tile([P, POOL_PAGES * DV], U8, name="vsc_pool", align_bytes=64)
-        nc.vector.memset(vsc_pool[:].bitcast(I32), 0)
         for quad in range(4):
             r = 32 * quad + V_SHIFT
             nc.sync.dma_start(

@@ -17,7 +17,7 @@ HALF = NQ // 2
 VS_ROW = P - 1
 Q_SHIFT = 4
 V_SHIFT = 8
-HEAD = 512
+HEAD = 1024
 
 FLOPS = 2 * NQ * N * D + 2 * NQ * N * DV
 
@@ -59,15 +59,15 @@ def tile_attend_pkv8q_silu_kernel(
 
         kw_hbm = k_words[0].rearrange("p n t -> p (n t)").bitcast(I32)
         nc.sync.dma_start(offs_t[:], offs)
-        nc.sync.dma_start(kw_pool[:, 0:HEAD], kw_hbm[:, 0:HEAD])
         nc.sync.dma_start(vs_pool[VS_ROW:P, :], vs[0:1, :])
-        nc.sync.dma_start(voffs_t[:], voffs)
+        nc.sync.dma_start(kw_pool[:, 0:HEAD], kw_hbm[:, 0:HEAD])
         for quad in (0, 2, 1, 3):
             nc.sync.dma_start(
                 ks_pool[32 * quad : 32 * quad + 4, :].bitcast(I32),
                 k_scales[0, 4 * quad : 4 * quad + 4, :].bitcast(I32),
             )
         nc.sync.dma_start(kw_pool[:, HEAD:T], kw_hbm[:, HEAD:T])
+        nc.sync.dma_start(voffs_t[:], voffs)
         nc.sync.dma_start(qw[:], q_words[0, 0].rearrange("p n t -> p (n t)").bitcast(I32))
         for quad in range(4):
             r = 32 * quad + Q_SHIFT
@@ -118,8 +118,6 @@ def tile_attend_pkv8q_silu_kernel(
                     start=True,
                     stop=True,
                 )
-        vw_g = sb.tile([P, PAGES * DV], U32, name="vw_g", align_bytes=64)
-        nc.vector.tensor_copy(vw_g[:], vw_pool[:].bitcast(U32).indirect(voffs_t[:]))
 
         w16 = [sb.tile([P, NQ, PACK], BF16, name=f"w16_{g}", align_bytes=64) for g in range(PAGES)]
         wq = [sb.tile([P, NQ], U32, name=f"wq{g}", align_bytes=64) for g in range(PAGES)]
@@ -143,8 +141,10 @@ def tile_attend_pkv8q_silu_kernel(
 
         weigh(0, 0)
         weigh(0, 1)
-        weigh(1, 0)
+        vw_g = sb.tile([P, PAGES * DV], U32, name="vw_g", tag="p32_00", align_bytes=64)
+        nc.vector.tensor_copy(vw_g[:], vw_pool[:].bitcast(U32).indirect(voffs_t[:]))
         quantize(0)
+        weigh(1, 0)
         weigh(1, 1)
         vsc_g = sb.tile([P, PAGES * DV], U8, name="vsc_g", tag="p32_10", align_bytes=64)
         nc.vector.tensor_copy(vsc_g[:], vsc_pool[:].indirect(voffs_t[:]))

@@ -17,7 +17,7 @@ HALF = NQ // 2
 VS_ROW = P - 1
 Q_SHIFT = 4
 V_SHIFT = 8
-HEAD = 1024
+HEAD = 512
 
 FLOPS = 2 * NQ * N * D + 2 * NQ * N * DV
 
@@ -58,14 +58,11 @@ def tile_attend_pkv8q_silu_kernel(
         make_identity(nc, ident[:])
 
         kw_hbm = k_words[0].rearrange("p n t -> p (n t)").bitcast(I32)
+        nc.sync.dma_start(kw_pool[:, 0:HEAD], kw_hbm[:, 0:HEAD])
         nc.sync.dma_start(offs_t[:], offs)
         nc.sync.dma_start(vs_pool[VS_ROW:P, :], vs[0:1, :])
-        nc.sync.dma_start(kw_pool[:, 0:HEAD], kw_hbm[:, 0:HEAD])
-        for quad in (0, 2, 1, 3):
-            nc.sync.dma_start(
-                ks_pool[32 * quad : 32 * quad + 4, :].bitcast(I32),
-                k_scales[0, 4 * quad : 4 * quad + 4, :].bitcast(I32),
-            )
+        for r in range(4):
+            nc.sync.dma_start(ks_pool[r:P:32, :].bitcast(I32), k_scales[0, r:16:4, :].bitcast(I32))
         nc.sync.dma_start(kw_pool[:, HEAD:T], kw_hbm[:, HEAD:T])
         nc.sync.dma_start(voffs_t[:], voffs)
         nc.sync.dma_start(qw[:], q_words[0, 0].rearrange("p n t -> p (n t)").bitcast(I32))
@@ -119,6 +116,9 @@ def tile_attend_pkv8q_silu_kernel(
                     stop=True,
                 )
 
+        vw_g = sb.tile([P, PAGES * DV], U32, name="vw_g", align_bytes=64)
+        nc.vector.tensor_copy(vw_g[:], vw_pool[:].bitcast(U32).indirect(voffs_t[:]))
+
         w16 = [sb.tile([P, NQ, PACK], BF16, name=f"w16_{g}", align_bytes=64) for g in range(PAGES)]
         wq = [sb.tile([P, NQ], U32, name=f"wq{g}", align_bytes=64) for g in range(PAGES)]
         wsc = [sb.tile([P, NQ], U8, name=f"wsc{g}", align_bytes=64) for g in range(PAGES)]
@@ -141,10 +141,8 @@ def tile_attend_pkv8q_silu_kernel(
 
         weigh(0, 0)
         weigh(0, 1)
-        vw_g = sb.tile([P, PAGES * DV], U32, name="vw_g", tag="p32_00", align_bytes=64)
-        nc.vector.tensor_copy(vw_g[:], vw_pool[:].bitcast(U32).indirect(voffs_t[:]))
-        quantize(0)
         weigh(1, 0)
+        quantize(0)
         weigh(1, 1)
         vsc_g = sb.tile([P, PAGES * DV], U8, name="vsc_g", tag="p32_10", align_bytes=64)
         nc.vector.tensor_copy(vsc_g[:], vsc_pool[:].indirect(voffs_t[:]))

@@ -1,7 +1,6 @@
 from contextlib import ExitStack
 
 import concourse.mybir as mybir
-from concourse.masks import make_identity
 
 P = 128
 T = 4096
@@ -15,9 +14,10 @@ D = 512
 PACK = 4
 HALF = NQ // 2
 VS_ROW = P - 1
-Q_SHIFT = 4
+S_ROW = P - 16
 V_SHIFT = 8
-HEAD = 512
+FILL_A = 841
+FILL_V = 1680
 
 FLOPS = 2 * NQ * N * D + 2 * NQ * N * DV
 
@@ -46,46 +46,25 @@ def tile_attend_pkv8q_silu_kernel(
         kw_pool = sb.tile([P, T], I32, name="kw_pool", align_bytes=64)
         ks_pool = sb.tile([P, T], U8, name="ks_pool", align_bytes=64)
         vs_pool = sb.tile([P, T], F32, name="vs_pool", align_bytes=64)
-        qw = sb.tile([P, NQ], I32, name="qw", align_bytes=64)
-        qs = sb.tile([P, NQ], U8, name="qs", align_bytes=64)
-        ident = sb.tile([P, P], F32, name="ident", align_bytes=64)
-
-        nc.vector.memset(ks_pool[:].bitcast(I32), 0)
-        nc.vector.memset(vs_pool[0:VS_ROW, :].bitcast(I32), 0)
-        nc.gpsimd.memset(qs[:].bitcast(I32), 0)
         vsc_pool = sb.tile([P, POOL_PAGES * DV], U8, name="vsc_pool", align_bytes=64)
-        nc.gpsimd.memset(vsc_pool[:].bitcast(I32), 0)
-        make_identity(nc, ident[:])
+        vw_pool = sb.tile([P, POOL_PAGES * DV], I32, name="vw_pool", align_bytes=64)
+        qw = sb.tile([P, NQ], I32, name="qw", align_bytes=64)
+        planes = sb.tile([P, N + NQ], U8, name="planes", align_bytes=64)
 
-        kw_hbm = k_words[0].rearrange("p n t -> p (n t)").bitcast(I32)
-        nc.sync.dma_start(kw_pool[:, 0:HEAD], kw_hbm[:, 0:HEAD])
+        nc.gpsimd.memset(ks_pool[0:S_ROW, :].bitcast(I32), 0)
+        nc.vector.memset(vs_pool[0:VS_ROW, 0:FILL_A].bitcast(I32), 0)
+        nc.vector.memset(vs_pool[0:VS_ROW, FILL_A:FILL_V].bitcast(I32), 0)
+        nc.gpsimd.memset(vs_pool[0:VS_ROW, FILL_V:T].bitcast(I32), 0)
+        nc.gpsimd.memset(vsc_pool[:].bitcast(I32), 0)
+        nc.gpsimd.memset(planes[0:S_ROW, N : N + NQ].bitcast(I32), 0)
+
+        nc.sync.dma_start(ks_pool[S_ROW:P, :].bitcast(I32), k_scales[0].bitcast(I32))
         nc.sync.dma_start(offs_t[:], offs)
         nc.sync.dma_start(vs_pool[VS_ROW:P, :], vs[0:1, :])
-        for r in range(4):
-            nc.sync.dma_start(ks_pool[r:P:32, :].bitcast(I32), k_scales[0, r:16:4, :].bitcast(I32))
-        nc.sync.dma_start(kw_pool[:, HEAD:T], kw_hbm[:, HEAD:T])
+        nc.sync.dma_start(planes[S_ROW:P, N : N + NQ].bitcast(I32), q_scales[0, 0].bitcast(I32))
         nc.sync.dma_start(voffs_t[:], voffs)
         nc.sync.dma_start(qw[:], q_words[0, 0].rearrange("p n t -> p (n t)").bitcast(I32))
-        for quad in range(4):
-            r = 32 * quad + Q_SHIFT
-            nc.sync.dma_start(qs[r : r + 4, :].bitcast(I32), q_scales[0, 0, 4 * quad : 4 * quad + 4, :].bitcast(I32))
-
-        vw_pool = sb.tile([P, POOL_PAGES * DV], I32, name="vw_pool", align_bytes=64)
-        nc.sync.dma_start(
-            vw_pool[:].rearrange("p (u e) -> p u e", u=POOL_PAGES),
-            v_words.rearrange("u p e t -> p u (e t)").bitcast(I32),
-        )
-
-        vs_g = sb.tile([P, N], F32, name="vs_g", align_bytes=64)
-        nc.vector.tensor_copy(vs_g[:], vs_pool[:].indirect(offs_t[:]))
-        vs_t = ps.tile([P, 2 * P], F32, name="vs_t")
-        for j in reversed(range(PAGES * PACK)):
-            g, t = divmod(j, PACK)
-            nc.tensor.transpose(vs_t[:, j + 1 : j + 1 + P], vs_g[:, g * PAGE + t : (g + 1) * PAGE : PACK], ident[:])
-
-        ks_g = sb.tile([P, N], U8, name="ks_g", align_bytes=64)
-        ks_p = sb.tile([P, N], U8, name="ks_p", align_bytes=64)
-        nc.vector.tensor_copy(ks_g[:], ks_pool[:].indirect(offs_t[:]))
+        nc.sync.dma_start(kw_pool[:], k_words[0].rearrange("p n t -> p (n t)").bitcast(I32))
         for quad in range(4):
             r = 32 * quad + V_SHIFT
             nc.sync.dma_start(
@@ -93,25 +72,46 @@ def tile_attend_pkv8q_silu_kernel(
                 v_scales[:, 4 * quad : 4 * quad + 4, :].bitcast(I32).rearrange("u r e -> r u e"),
             )
 
+        ks_g = sb.tile([P, N], U8, name="ks_g", align_bytes=64)
+        vs_g = [sb.tile([P, PAGE], F32, name=f"vs_g{g}", align_bytes=64) for g in range(PAGES)]
+        vs_t = [sb.tile([P, PACK], F32, name=f"vs_t{g}", align_bytes=64) for g in range(PAGES)]
+
+        def page_offs(g):
+            return offs_t[:, g * (PAGE // 16) : (g + 1) * (PAGE // 16)]
+
+        def token_scales(g):
+            nc.vector.tensor_copy(vs_g[g][:], vs_pool[:].indirect(page_offs(g)))
+            nc.sync.dma_start(vs_t[g][:], vs_g[g][VS_ROW:P, :].rearrange("p (s t) -> p s t", t=PACK))
+
+        nc.vector.tensor_copy(ks_g[:], ks_pool[:].indirect(offs_t[:]))
+        token_scales(0)
         nc.vector.tensor_copy(
-            ks_p[:].rearrange("p (g t s) -> p g t s", g=PAGES, t=PACK),
+            planes[:, 0:N].rearrange("p (g t s) -> p g t s", g=PAGES, t=PACK),
             ks_g[:].rearrange("p (g s t) -> p g t s", g=PAGES, t=PACK),
         )
+        for r in range(4):
+            nc.sync.dma_start(planes[r:P:32, :].bitcast(I32), planes[S_ROW + r : P : 4, :].bitcast(I32))
+        nc.sync.dma_start(
+            vw_pool[:].rearrange("p (u e) -> p u e", u=POOL_PAGES),
+            v_words.rearrange("u p e t -> p u (e t)").bitcast(I32),
+        )
+        token_scales(1)
+
         kw_g = sb.tile([P, N], U32, name="kw_g", align_bytes=64)
         score = [ps.tile([P, PACK, NQ], F32, name=f"score{g}") for g in range(PAGES)]
         for g in range(PAGES):
             nc.vector.tensor_copy(
                 kw_g[:, g * PAGE : (g + 1) * PAGE].rearrange("p (t s) -> p s t", t=PACK),
-                kw_pool[:].bitcast(U32).indirect(offs_t[:, g * (PAGE // 16) : (g + 1) * (PAGE // 16)]),
+                kw_pool[:].bitcast(U32).indirect(page_offs(g)),
             )
             for t in range(PACK):
                 slots = slice(g * PAGE + t * P, g * PAGE + (t + 1) * P)
                 nc.tensor.matmul_mx(
                     out=score[g][:, t, :],
                     lhsT=kw_g[:, slots].bitcast(FP8X4),
-                    lhsT_scale=ks_p[:, slots],
+                    lhsT_scale=planes[:, slots],
                     rhs=qw[:].bitcast(FP8X4),
-                    rhs_scale=qs[Q_SHIFT:P, :],
+                    rhs_scale=planes[:, N : N + NQ],
                     start=True,
                     stop=True,
                 )
@@ -130,7 +130,7 @@ def tile_attend_pkv8q_silu_kernel(
             nc.vector.tensor_tensor(
                 w16[g][:, cols, :],
                 p32[:],
-                vs_t[:, P + g * PACK : P + (g + 1) * PACK].unsqueeze(1).to_broadcast([P, HALF, PACK]),
+                vs_t[g][:].unsqueeze(1).to_broadcast([P, HALF, PACK]),
                 MULT,
             )
 

@@ -14,10 +14,10 @@ D = 512
 PACK = 4
 HALF = NQ // 2
 VS_ROW = P - 1
-S_ROW = P - 16
-V_SHIFT = 8
-FILL_A = 841
-FILL_V = 1680
+SPREAD = 8
+Q_COL = N
+V_COL = N + NQ
+HEAD = 640
 
 FLOPS = 2 * NQ * N * D + 2 * NQ * N * DV
 
@@ -49,53 +49,51 @@ def tile_attend_pkv8q_silu_kernel(
         vsc_pool = sb.tile([P, POOL_PAGES * DV], U8, name="vsc_pool", align_bytes=64)
         vw_pool = sb.tile([P, POOL_PAGES * DV], I32, name="vw_pool", align_bytes=64)
         qw = sb.tile([P, NQ], I32, name="qw", align_bytes=64)
-        planes = sb.tile([P, N + NQ], U8, name="planes", align_bytes=64)
+        planes = sb.tile([P, V_COL + PAGES * DV], U8, name="planes", align_bytes=64)
 
-        nc.gpsimd.memset(ks_pool[0:S_ROW, :].bitcast(I32), 0)
-        nc.vector.memset(vs_pool[0:VS_ROW, 0:FILL_A].bitcast(I32), 0)
-        nc.vector.memset(vs_pool[0:VS_ROW, FILL_A:FILL_V].bitcast(I32), 0)
-        nc.gpsimd.memset(vs_pool[0:VS_ROW, FILL_V:T].bitcast(I32), 0)
-        nc.gpsimd.memset(vsc_pool[:].bitcast(I32), 0)
-        nc.gpsimd.memset(planes[0:S_ROW, N : N + NQ].bitcast(I32), 0)
+        nc.vector.memset(vsc_pool[:].bitcast(I32), 0)
+        nc.vector.memset(planes[:, Q_COL:V_COL].bitcast(I32), 0)
+        nc.vector.memset(ks_pool[:].bitcast(I32), 0)
+        nc.vector.memset(vs_pool[0:VS_ROW, :].bitcast(I32), 0)
 
-        nc.sync.dma_start(ks_pool[S_ROW:P, :].bitcast(I32), k_scales[0].bitcast(I32))
+        kw_hbm = k_words[0].rearrange("p n t -> p (n t)").bitcast(I32)
+        nc.sync.dma_start(kw_pool[:, 0:HEAD], kw_hbm[:, 0:HEAD])
         nc.sync.dma_start(offs_t[:], offs)
-        nc.sync.dma_start(vs_pool[VS_ROW:P, :], vs[0:1, :])
-        nc.sync.dma_start(planes[S_ROW:P, N : N + NQ].bitcast(I32), q_scales[0, 0].bitcast(I32))
         nc.sync.dma_start(voffs_t[:], voffs)
+        nc.sync.dma_start(
+            vsc_pool[0:P:SPREAD, :].bitcast(I32).rearrange("r (u e) -> r u e", u=POOL_PAGES),
+            v_scales.bitcast(I32).rearrange("u r e -> r u e"),
+        )
+        nc.sync.dma_start(planes[0:P:SPREAD, Q_COL:V_COL].bitcast(I32), q_scales[0, 0].bitcast(I32))
+        nc.sync.dma_start(ks_pool[0:P:SPREAD, :].bitcast(I32), k_scales[0].bitcast(I32))
+        nc.sync.dma_start(vs_pool[VS_ROW:P, :], vs[0:1, :])
+        nc.sync.dma_start(kw_pool[:, HEAD:T], kw_hbm[:, HEAD:T])
         nc.sync.dma_start(qw[:], q_words[0, 0].rearrange("p n t -> p (n t)").bitcast(I32))
-        nc.sync.dma_start(kw_pool[:], k_words[0].rearrange("p n t -> p (n t)").bitcast(I32))
-        for quad in range(4):
-            r = 32 * quad + V_SHIFT
-            nc.sync.dma_start(
-                vsc_pool[r : r + 4, :].bitcast(I32).rearrange("r (u e) -> r u e", u=POOL_PAGES),
-                v_scales[:, 4 * quad : 4 * quad + 4, :].bitcast(I32).rearrange("u r e -> r u e"),
-            )
+        nc.sync.dma_start(
+            vw_pool[:].rearrange("p (u e) -> p u e", u=POOL_PAGES),
+            v_words.rearrange("u p e t -> p u (e t)").bitcast(I32),
+        )
 
         ks_g = sb.tile([P, N], U8, name="ks_g", align_bytes=64)
+        vsc_g = sb.tile([P, PAGES * DV], U8, name="vsc_g", align_bytes=64)
         vs_g = [sb.tile([P, PAGE], F32, name=f"vs_g{g}", align_bytes=64) for g in range(PAGES)]
         vs_t = [sb.tile([P, PACK], F32, name=f"vs_t{g}", align_bytes=64) for g in range(PAGES)]
 
         def page_offs(g):
             return offs_t[:, g * (PAGE // 16) : (g + 1) * (PAGE // 16)]
 
-        def token_scales(g):
-            nc.vector.tensor_copy(vs_g[g][:], vs_pool[:].indirect(page_offs(g)))
-            nc.sync.dma_start(vs_t[g][:], vs_g[g][VS_ROW:P, :].rearrange("p (s t) -> p s t", t=PACK))
-
         nc.vector.tensor_copy(ks_g[:], ks_pool[:].indirect(offs_t[:]))
-        token_scales(0)
+        nc.vector.tensor_copy(vsc_g[:], vsc_pool[:].indirect(voffs_t[:]))
         nc.vector.tensor_copy(
             planes[:, 0:N].rearrange("p (g t s) -> p g t s", g=PAGES, t=PACK),
             ks_g[:].rearrange("p (g s t) -> p g t s", g=PAGES, t=PACK),
         )
-        for r in range(4):
-            nc.sync.dma_start(planes[r:P:32, :].bitcast(I32), planes[S_ROW + r : P : 4, :].bitcast(I32))
-        nc.sync.dma_start(
-            vw_pool[:].rearrange("p (u e) -> p u e", u=POOL_PAGES),
-            v_words.rearrange("u p e t -> p u (e t)").bitcast(I32),
-        )
-        token_scales(1)
+        nc.vector.tensor_copy(planes[:, V_COL:].bitcast(I32), vsc_g[:].bitcast(I32))
+        for r in range(1, 4):
+            nc.scalar.dma_start(planes[r:P:32, :].bitcast(I32), planes[SPREAD * r : P : 32, :].bitcast(I32))
+        for g in range(PAGES):
+            nc.vector.tensor_copy(vs_g[g][:], vs_pool[:].indirect(page_offs(g)))
+            nc.scalar.dma_start(vs_t[g][:], vs_g[g][VS_ROW:P, :].rearrange("p (s t) -> p s t", t=PACK))
 
         kw_g = sb.tile([P, N], U32, name="kw_g", align_bytes=64)
         score = [ps.tile([P, PACK, NQ], F32, name=f"score{g}") for g in range(PAGES)]
@@ -111,7 +109,7 @@ def tile_attend_pkv8q_silu_kernel(
                     lhsT=kw_g[:, slots].bitcast(FP8X4),
                     lhsT_scale=planes[:, slots],
                     rhs=qw[:].bitcast(FP8X4),
-                    rhs_scale=planes[:, N : N + NQ],
+                    rhs_scale=planes[:, Q_COL:V_COL],
                     start=True,
                     stop=True,
                 )
@@ -142,10 +140,8 @@ def tile_attend_pkv8q_silu_kernel(
         weigh(0, 0)
         weigh(0, 1)
         weigh(1, 0)
-        quantize(0)
         weigh(1, 1)
-        vsc_g = sb.tile([P, PAGES * DV], U8, name="vsc_g", tag="p32_10", align_bytes=64)
-        nc.vector.tensor_copy(vsc_g[:], vsc_pool[:].indirect(voffs_t[:]))
+        quantize(0)
         quantize(1)
 
         acc = ps.tile([P, DV], F32, name="acc")
@@ -155,7 +151,7 @@ def tile_attend_pkv8q_silu_kernel(
                 lhsT=wq[g][:].bitcast(FP8X4),
                 lhsT_scale=wsc[g][:],
                 rhs=vw_g[:, g * DV : (g + 1) * DV].bitcast(FP8X4),
-                rhs_scale=vsc_g[V_SHIFT:P, g * DV : (g + 1) * DV],
+                rhs_scale=planes[:, V_COL + g * DV : V_COL + (g + 1) * DV],
                 start=(g == 0),
                 stop=(g == PAGES - 1),
             )

@@ -15,8 +15,7 @@ PACK = 4
 HALF = NQ // 2
 VS_ROW = P - 1
 SPREAD = 8
-Q_COL = N
-V_COL = N + NQ
+V_SHIFT = 8
 HEAD = 640
 
 FLOPS = 2 * NQ * N * D + 2 * NQ * N * DV
@@ -49,10 +48,9 @@ def tile_attend_pkv8q_silu_kernel(
         vsc_pool = sb.tile([P, POOL_PAGES * DV], U8, name="vsc_pool", align_bytes=64)
         vw_pool = sb.tile([P, POOL_PAGES * DV], I32, name="vw_pool", align_bytes=64)
         qw = sb.tile([P, NQ], I32, name="qw", align_bytes=64)
-        planes = sb.tile([P, V_COL + PAGES * DV], U8, name="planes", align_bytes=64)
+        planes = sb.tile([P, N + NQ], U8, name="planes", align_bytes=64)
 
-        nc.vector.memset(vsc_pool[:].bitcast(I32), 0)
-        nc.vector.memset(planes[:, Q_COL:V_COL].bitcast(I32), 0)
+        nc.vector.memset(planes[:, N:].bitcast(I32), 0)
         nc.vector.memset(ks_pool[:].bitcast(I32), 0)
         nc.vector.memset(vs_pool[0:VS_ROW, :].bitcast(I32), 0)
 
@@ -60,40 +58,43 @@ def tile_attend_pkv8q_silu_kernel(
         nc.sync.dma_start(kw_pool[:, 0:HEAD], kw_hbm[:, 0:HEAD])
         nc.sync.dma_start(offs_t[:], offs)
         nc.sync.dma_start(voffs_t[:], voffs)
-        nc.sync.dma_start(
-            vsc_pool[0:P:SPREAD, :].bitcast(I32).rearrange("r (u e) -> r u e", u=POOL_PAGES),
-            v_scales.bitcast(I32).rearrange("u r e -> r u e"),
-        )
-        nc.sync.dma_start(planes[0:P:SPREAD, Q_COL:V_COL].bitcast(I32), q_scales[0, 0].bitcast(I32))
+        nc.sync.dma_start(planes[0:P:SPREAD, N:].bitcast(I32), q_scales[0, 0].bitcast(I32))
         nc.sync.dma_start(ks_pool[0:P:SPREAD, :].bitcast(I32), k_scales[0].bitcast(I32))
         nc.sync.dma_start(vs_pool[VS_ROW:P, :], vs[0:1, :])
         nc.sync.dma_start(kw_pool[:, HEAD:T], kw_hbm[:, HEAD:T])
         nc.sync.dma_start(qw[:], q_words[0, 0].rearrange("p n t -> p (n t)").bitcast(I32))
-        nc.sync.dma_start(
-            vw_pool[:].rearrange("p (u e) -> p u e", u=POOL_PAGES),
-            v_words.rearrange("u p e t -> p u (e t)").bitcast(I32),
-        )
 
         ks_g = sb.tile([P, N], U8, name="ks_g", align_bytes=64)
-        vsc_g = sb.tile([P, PAGES * DV], U8, name="vsc_g", align_bytes=64)
         vs_g = [sb.tile([P, PAGE], F32, name=f"vs_g{g}", align_bytes=64) for g in range(PAGES)]
         vs_t = [sb.tile([P, PACK], F32, name=f"vs_t{g}", align_bytes=64) for g in range(PAGES)]
 
         def page_offs(g):
             return offs_t[:, g * (PAGE // 16) : (g + 1) * (PAGE // 16)]
 
+        def token_scales(g):
+            nc.vector.tensor_copy(vs_g[g][:], vs_pool[:].indirect(page_offs(g)))
+            nc.sync.dma_start(vs_t[g][:], vs_g[g][VS_ROW:P, :].rearrange("p (s t) -> p s t", t=PACK))
+
         nc.vector.tensor_copy(ks_g[:], ks_pool[:].indirect(offs_t[:]))
-        nc.vector.tensor_copy(vsc_g[:], vsc_pool[:].indirect(voffs_t[:]))
+        nc.vector.memset(vsc_pool[:].bitcast(I32), 0)
         nc.vector.tensor_copy(
             planes[:, 0:N].rearrange("p (g t s) -> p g t s", g=PAGES, t=PACK),
             ks_g[:].rearrange("p (g s t) -> p g t s", g=PAGES, t=PACK),
         )
-        nc.vector.tensor_copy(planes[:, V_COL:].bitcast(I32), vsc_g[:].bitcast(I32))
         for r in range(1, 4):
-            nc.scalar.dma_start(planes[r:P:32, :].bitcast(I32), planes[SPREAD * r : P : 32, :].bitcast(I32))
-        for g in range(PAGES):
-            nc.vector.tensor_copy(vs_g[g][:], vs_pool[:].indirect(page_offs(g)))
-            nc.scalar.dma_start(vs_t[g][:], vs_g[g][VS_ROW:P, :].rearrange("p (s t) -> p s t", t=PACK))
+            nc.sync.dma_start(planes[r:P:32, :].bitcast(I32), planes[SPREAD * r : P : 32, :].bitcast(I32))
+        token_scales(0)
+        nc.sync.dma_start(
+            vw_pool[:].rearrange("p (u e) -> p u e", u=POOL_PAGES),
+            v_words.rearrange("u p e t -> p u (e t)").bitcast(I32),
+        )
+        token_scales(1)
+        for quad in range(4):
+            r = 32 * quad + V_SHIFT
+            nc.sync.dma_start(
+                vsc_pool[r : r + 4, :].bitcast(I32).rearrange("r (u e) -> r u e", u=POOL_PAGES),
+                v_scales[:, 4 * quad : 4 * quad + 4, :].bitcast(I32).rearrange("u r e -> r u e"),
+            )
 
         kw_g = sb.tile([P, N], U32, name="kw_g", align_bytes=64)
         score = [ps.tile([P, PACK, NQ], F32, name=f"score{g}") for g in range(PAGES)]
@@ -109,7 +110,7 @@ def tile_attend_pkv8q_silu_kernel(
                     lhsT=kw_g[:, slots].bitcast(FP8X4),
                     lhsT_scale=planes[:, slots],
                     rhs=qw[:].bitcast(FP8X4),
-                    rhs_scale=planes[:, Q_COL:V_COL],
+                    rhs_scale=planes[:, N:],
                     start=True,
                     stop=True,
                 )
@@ -140,8 +141,10 @@ def tile_attend_pkv8q_silu_kernel(
         weigh(0, 0)
         weigh(0, 1)
         weigh(1, 0)
-        weigh(1, 1)
         quantize(0)
+        weigh(1, 1)
+        vsc_g = sb.tile([P, PAGES * DV], U8, name="vsc_g", tag="p32_10", align_bytes=64)
+        nc.vector.tensor_copy(vsc_g[:], vsc_pool[:].indirect(voffs_t[:]))
         quantize(1)
 
         acc = ps.tile([P, DV], F32, name="acc")
@@ -151,7 +154,7 @@ def tile_attend_pkv8q_silu_kernel(
                 lhsT=wq[g][:].bitcast(FP8X4),
                 lhsT_scale=wsc[g][:],
                 rhs=vw_g[:, g * DV : (g + 1) * DV].bitcast(FP8X4),
-                rhs_scale=planes[:, V_COL + g * DV : V_COL + (g + 1) * DV],
+                rhs_scale=vsc_g[V_SHIFT:P, g * DV : (g + 1) * DV],
                 start=(g == 0),
                 stop=(g == PAGES - 1),
             )

@@ -15,8 +15,8 @@ PACK = 4
 HALF = NQ // 2
 VS_ROW = P - 1
 SPREAD = 8
-V_SHIFT = 8
-HEAD = 640
+Q_COL = N
+V_COL = N + NQ
 
 FLOPS = 2 * NQ * N * D + 2 * NQ * N * DV
 
@@ -48,53 +48,49 @@ def tile_attend_pkv8q_silu_kernel(
         vsc_pool = sb.tile([P, POOL_PAGES * DV], U8, name="vsc_pool", align_bytes=64)
         vw_pool = sb.tile([P, POOL_PAGES * DV], I32, name="vw_pool", align_bytes=64)
         qw = sb.tile([P, NQ], I32, name="qw", align_bytes=64)
-        planes = sb.tile([P, N + NQ], U8, name="planes", align_bytes=64)
+        planes = sb.tile([P, V_COL + PAGES * DV], U8, name="planes", align_bytes=64)
 
-        nc.vector.memset(planes[:, N:].bitcast(I32), 0)
+        nc.vector.memset(planes[:, Q_COL:V_COL].bitcast(I32), 0)
+        nc.vector.memset(vsc_pool[:].bitcast(I32), 0)
         nc.vector.memset(ks_pool[:].bitcast(I32), 0)
         nc.vector.memset(vs_pool[0:VS_ROW, :].bitcast(I32), 0)
 
-        kw_hbm = k_words[0].rearrange("p n t -> p (n t)").bitcast(I32)
-        nc.sync.dma_start(kw_pool[:, 0:HEAD], kw_hbm[:, 0:HEAD])
+        nc.sync.dma_start(vs_pool[VS_ROW:P, :], vs[0:1, :])
         nc.sync.dma_start(offs_t[:], offs)
         nc.sync.dma_start(voffs_t[:], voffs)
-        nc.sync.dma_start(planes[0:P:SPREAD, N:].bitcast(I32), q_scales[0, 0].bitcast(I32))
-        nc.sync.dma_start(ks_pool[0:P:SPREAD, :].bitcast(I32), k_scales[0].bitcast(I32))
-        nc.sync.dma_start(vs_pool[VS_ROW:P, :], vs[0:1, :])
-        nc.sync.dma_start(kw_pool[:, HEAD:T], kw_hbm[:, HEAD:T])
+        nc.sync.dma_start(planes[0:P:SPREAD, Q_COL:V_COL].bitcast(I32), q_scales[0, 0].bitcast(I32))
+        nc.sync.dma_start(
+            vsc_pool[0:P:SPREAD, :].bitcast(I32).rearrange("r (u e) -> r u e", u=POOL_PAGES),
+            v_scales.bitcast(I32).rearrange("u r e -> r u e"),
+        )
         nc.sync.dma_start(qw[:], q_words[0, 0].rearrange("p n t -> p (n t)").bitcast(I32))
+        nc.sync.dma_start(ks_pool[0:P:SPREAD, :].bitcast(I32), k_scales[0].bitcast(I32))
+        nc.sync.dma_start(kw_pool[:], k_words[0].rearrange("p n t -> p (n t)").bitcast(I32))
 
         ks_g = sb.tile([P, N], U8, name="ks_g", align_bytes=64)
+        vsc_g = sb.tile([P, PAGES * DV], U8, name="vsc_g", align_bytes=64)
         vs_g = [sb.tile([P, PAGE], F32, name=f"vs_g{g}", align_bytes=64) for g in range(PAGES)]
         vs_t = [sb.tile([P, PACK], F32, name=f"vs_t{g}", align_bytes=64) for g in range(PAGES)]
 
         def page_offs(g):
             return offs_t[:, g * (PAGE // 16) : (g + 1) * (PAGE // 16)]
 
-        def token_scales(g):
-            nc.vector.tensor_copy(vs_g[g][:], vs_pool[:].indirect(page_offs(g)))
-            nc.sync.dma_start(vs_t[g][:], vs_g[g][VS_ROW:P, :].rearrange("p (s t) -> p s t", t=PACK))
-
+        nc.vector.tensor_copy(vsc_g[:], vsc_pool[:].indirect(voffs_t[:]))
         nc.vector.tensor_copy(ks_g[:], ks_pool[:].indirect(offs_t[:]))
-        nc.vector.memset(vsc_pool[:].bitcast(I32), 0)
+        nc.vector.tensor_copy(planes[:, V_COL:].bitcast(I32), vsc_g[:].bitcast(I32))
         nc.vector.tensor_copy(
             planes[:, 0:N].rearrange("p (g t s) -> p g t s", g=PAGES, t=PACK),
             ks_g[:].rearrange("p (g s t) -> p g t s", g=PAGES, t=PACK),
         )
         for r in range(1, 4):
             nc.sync.dma_start(planes[r:P:32, :].bitcast(I32), planes[SPREAD * r : P : 32, :].bitcast(I32))
-        token_scales(0)
         nc.sync.dma_start(
             vw_pool[:].rearrange("p (u e) -> p u e", u=POOL_PAGES),
             v_words.rearrange("u p e t -> p u (e t)").bitcast(I32),
         )
-        token_scales(1)
-        for quad in range(4):
-            r = 32 * quad + V_SHIFT
-            nc.sync.dma_start(
-                vsc_pool[r : r + 4, :].bitcast(I32).rearrange("r (u e) -> r u e", u=POOL_PAGES),
-                v_scales[:, 4 * quad : 4 * quad + 4, :].bitcast(I32).rearrange("u r e -> r u e"),
-            )
+        for g in range(PAGES):
+            nc.vector.tensor_copy(vs_g[g][:], vs_pool[:].indirect(page_offs(g)))
+            nc.sync.dma_start(vs_t[g][:], vs_g[g][VS_ROW:P, :].rearrange("p (s t) -> p s t", t=PACK))
 
         kw_g = sb.tile([P, N], U32, name="kw_g", align_bytes=64)
         score = [ps.tile([P, PACK, NQ], F32, name=f"score{g}") for g in range(PAGES)]
@@ -110,7 +106,7 @@ def tile_attend_pkv8q_silu_kernel(
                     lhsT=kw_g[:, slots].bitcast(FP8X4),
                     lhsT_scale=planes[:, slots],
                     rhs=qw[:].bitcast(FP8X4),
-                    rhs_scale=planes[:, N:],
+                    rhs_scale=planes[:, Q_COL:V_COL],
                     start=True,
                     stop=True,
                 )
@@ -143,8 +139,6 @@ def tile_attend_pkv8q_silu_kernel(
         weigh(1, 0)
         quantize(0)
         weigh(1, 1)
-        vsc_g = sb.tile([P, PAGES * DV], U8, name="vsc_g", tag="p32_10", align_bytes=64)
-        nc.vector.tensor_copy(vsc_g[:], vsc_pool[:].indirect(voffs_t[:]))
         quantize(1)
 
         acc = ps.tile([P, DV], F32, name="acc")
@@ -154,7 +148,7 @@ def tile_attend_pkv8q_silu_kernel(
                 lhsT=wq[g][:].bitcast(FP8X4),
                 lhsT_scale=wsc[g][:],
                 rhs=vw_g[:, g * DV : (g + 1) * DV].bitcast(FP8X4),
-                rhs_scale=vsc_g[V_SHIFT:P, g * DV : (g + 1) * DV],
+                rhs_scale=planes[:, V_COL + g * DV : V_COL + (g + 1) * DV],
                 start=(g == 0),
                 stop=(g == PAGES - 1),
             )

@@ -67,30 +67,31 @@ def tile_attend_pkv8q_silu_kernel(
         nc.sync.dma_start(ks_pool[0:P:SPREAD, :].bitcast(I32), k_scales[0].bitcast(I32))
         nc.sync.dma_start(kw_pool[:], k_words[0].rearrange("p n t -> p (n t)").bitcast(I32))
 
-        ks_g = sb.tile([P, N], U8, name="ks_g", align_bytes=64)
+        ks_g = sb.tile([P, N], U8, name="ks_g", tag="gathered", align_bytes=64)
         vsc_g = sb.tile([P, PAGES * DV], U8, name="vsc_g", align_bytes=64)
-        vs_g = [sb.tile([P, PAGE], F32, name=f"vs_g{g}", align_bytes=64) for g in range(PAGES)]
         vs_t = [sb.tile([P, PACK], F32, name=f"vs_t{g}", align_bytes=64) for g in range(PAGES)]
 
         def page_offs(g):
             return offs_t[:, g * (PAGE // 16) : (g + 1) * (PAGE // 16)]
 
-        nc.vector.tensor_copy(vsc_g[:], vsc_pool[:].indirect(voffs_t[:]))
         nc.vector.tensor_copy(ks_g[:], ks_pool[:].indirect(offs_t[:]))
-        nc.vector.tensor_copy(planes[:, V_COL:].bitcast(I32), vsc_g[:].bitcast(I32))
+        nc.vector.tensor_copy(vsc_g[:], vsc_pool[:].indirect(voffs_t[:]))
         nc.vector.tensor_copy(
             planes[:, 0:N].rearrange("p (g t s) -> p g t s", g=PAGES, t=PACK),
             ks_g[:].rearrange("p (g s t) -> p g t s", g=PAGES, t=PACK),
         )
+        nc.vector.tensor_copy(planes[:, V_COL:].bitcast(I32), vsc_g[:].bitcast(I32))
         for r in range(1, 4):
             nc.sync.dma_start(planes[r:P:32, :].bitcast(I32), planes[SPREAD * r : P : 32, :].bitcast(I32))
         nc.sync.dma_start(
             vw_pool[:].rearrange("p (u e) -> p u e", u=POOL_PAGES),
             v_words.rearrange("u p e t -> p u (e t)").bitcast(I32),
         )
+        vs_g = sb.tile([P, N], F32, name="vs_g", tag="gathered", align_bytes=64)
         for g in range(PAGES):
-            nc.vector.tensor_copy(vs_g[g][:], vs_pool[:].indirect(page_offs(g)))
-            nc.sync.dma_start(vs_t[g][:], vs_g[g][VS_ROW:P, :].rearrange("p (s t) -> p s t", t=PACK))
+            page = slice(g * PAGE, (g + 1) * PAGE)
+            nc.vector.tensor_copy(vs_g[:, page], vs_pool[:].indirect(page_offs(g)))
+            nc.sync.dma_start(vs_t[g][:], vs_g[VS_ROW:P, page].rearrange("p (s t) -> p s t", t=PACK))
 
         kw_g = sb.tile([P, N], U32, name="kw_g", align_bytes=64)
         score = [ps.tile([P, PACK, NQ], F32, name=f"score{g}") for g in range(PAGES)]

@@ -15,6 +15,7 @@ PACK = 4
 HALF = NQ // 2
 VS_ROW = P - 1
 SPREAD = 8
+HEAD = 704
 Q_COL = N
 V_COL = N + NQ
 
@@ -50,22 +51,24 @@ def tile_attend_pkv8q_silu_kernel(
         qw = sb.tile([P, NQ], I32, name="qw", align_bytes=64)
         planes = sb.tile([P, V_COL + PAGES * DV], U8, name="planes", align_bytes=64)
 
-        nc.vector.memset(planes[:, Q_COL:V_COL].bitcast(I32), 0)
-        nc.vector.memset(vsc_pool[:].bitcast(I32), 0)
         nc.vector.memset(ks_pool[:].bitcast(I32), 0)
+        nc.vector.memset(vsc_pool[:].bitcast(I32), 0)
+        nc.vector.memset(planes[:, Q_COL:V_COL].bitcast(I32), 0)
         nc.vector.memset(vs_pool[0:VS_ROW, :].bitcast(I32), 0)
 
-        nc.sync.dma_start(vs_pool[VS_ROW:P, :], vs[0:1, :])
+        kw_hbm = k_words[0].rearrange("p n t -> p (n t)").bitcast(I32)
+        nc.sync.dma_start(kw_pool[:, 0:HEAD], kw_hbm[:, 0:HEAD])
         nc.sync.dma_start(offs_t[:], offs)
         nc.sync.dma_start(voffs_t[:], voffs)
-        nc.sync.dma_start(planes[0:P:SPREAD, Q_COL:V_COL].bitcast(I32), q_scales[0, 0].bitcast(I32))
+        nc.sync.dma_start(ks_pool[0:P:SPREAD, :].bitcast(I32), k_scales[0].bitcast(I32))
         nc.sync.dma_start(
             vsc_pool[0:P:SPREAD, :].bitcast(I32).rearrange("r (u e) -> r u e", u=POOL_PAGES),
             v_scales.bitcast(I32).rearrange("u r e -> r u e"),
         )
+        nc.sync.dma_start(planes[0:P:SPREAD, Q_COL:V_COL].bitcast(I32), q_scales[0, 0].bitcast(I32))
+        nc.sync.dma_start(vs_pool[VS_ROW:P, :], vs[0:1, :])
+        nc.sync.dma_start(kw_pool[:, HEAD:T], kw_hbm[:, HEAD:T])
         nc.sync.dma_start(qw[:], q_words[0, 0].rearrange("p n t -> p (n t)").bitcast(I32))
-        nc.sync.dma_start(ks_pool[0:P:SPREAD, :].bitcast(I32), k_scales[0].bitcast(I32))
-        nc.sync.dma_start(kw_pool[:], k_words[0].rearrange("p n t -> p (n t)").bitcast(I32))
 
         ks_g = sb.tile([P, N], U8, name="ks_g", tag="gathered", align_bytes=64)
         vsc_g = sb.tile([P, PAGES * DV], U8, name="vsc_g", align_bytes=64)
@@ -116,7 +119,6 @@ def tile_attend_pkv8q_silu_kernel(
         nc.vector.tensor_copy(vw_g[:], vw_pool[:].bitcast(U32).indirect(voffs_t[:]))
 
         w16 = [sb.tile([P, NQ, PACK], BF16, name=f"w16_{g}", align_bytes=64) for g in range(PAGES)]
-        wq = [sb.tile([P, NQ], U32, name=f"wq{g}", align_bytes=64) for g in range(PAGES)]
         wsc = [sb.tile([P, NQ], U8, name=f"wsc{g}", align_bytes=64) for g in range(PAGES)]
 
         def weigh(g, h):
@@ -130,17 +132,23 @@ def tile_attend_pkv8q_silu_kernel(
                 MULT,
             )
 
-        def quantize(g):
+        def quantize(g, cols):
             nc.vector.quantize_mx(
-                out=wq[g][:].bitcast(FP8X4), scales=wsc[g][:], in_=w16[g][:].rearrange("p q t -> p (q t)")
+                out=wq[g][:, cols].bitcast(FP8X4),
+                scales=wsc[g][:, cols],
+                in_=w16[g][:, cols, :].rearrange("p q t -> p (q t)"),
             )
 
-        weigh(0, 0)
-        weigh(0, 1)
-        weigh(1, 0)
-        quantize(0)
-        weigh(1, 1)
-        quantize(1)
+        for g in range(PAGES):
+            for h in range(2):
+                weigh(g, h)
+        wq = [
+            sb.tile([P, NQ], U32, name="wq0", tag="p32_10", align_bytes=64),
+            sb.tile([P, NQ], U32, name="wq1", align_bytes=64),
+        ]
+        quantize(0, slice(0, NQ))
+        quantize(1, slice(0, HALF))
+        quantize(1, slice(HALF, NQ))
 
         acc = ps.tile([P, DV], F32, name="acc")
         for g in range(PAGES):

@@ -16,6 +16,7 @@ HALF = NQ // 2
 VS_ROW = P - 1
 SPREAD = 8
 HEAD = 704
+V_EARLY = 3
 Q_COL = N
 V_COL = N + NQ
 
@@ -69,6 +70,9 @@ def tile_attend_pkv8q_silu_kernel(
         nc.sync.dma_start(vs_pool[VS_ROW:P, :], vs[0:1, :])
         nc.sync.dma_start(kw_pool[:, HEAD:T], kw_hbm[:, HEAD:T])
         nc.sync.dma_start(qw[:], q_words[0, 0].rearrange("p n t -> p (n t)").bitcast(I32))
+        vw_sb = vw_pool[:].rearrange("p (u e) -> p u e", u=POOL_PAGES)
+        vw_hbm = v_words.rearrange("u p e t -> p u (e t)").bitcast(I32)
+        nc.sync.dma_start(vw_sb[:, 0:V_EARLY, :], vw_hbm[:, 0:V_EARLY, :])
 
         ks_g = sb.tile([P, N], U8, name="ks_g", tag="gathered", align_bytes=64)
         vsc_g = sb.tile([P, PAGES * DV], U8, name="vsc_g", align_bytes=64)
@@ -86,10 +90,7 @@ def tile_attend_pkv8q_silu_kernel(
         nc.vector.tensor_copy(planes[:, V_COL:].bitcast(I32), vsc_g[:].bitcast(I32))
         for r in range(1, 4):
             nc.sync.dma_start(planes[r:P:32, :].bitcast(I32), planes[SPREAD * r : P : 32, :].bitcast(I32))
-        nc.sync.dma_start(
-            vw_pool[:].rearrange("p (u e) -> p u e", u=POOL_PAGES),
-            v_words.rearrange("u p e t -> p u (e t)").bitcast(I32),
-        )
+        nc.sync.dma_start(vw_sb[:, V_EARLY:, :], vw_hbm[:, V_EARLY:, :])
         vs_g = sb.tile([P, N], F32, name="vs_g", tag="gathered", align_bytes=64)
         for g in range(PAGES):
             page = slice(g * PAGE, (g + 1) * PAGE)

@@ -15,8 +15,8 @@ PACK = 4
 HALF = NQ // 2
 VS_ROW = P - 1
 SPREAD = 8
-HEAD = 704
 V_EARLY = 3
+FILL_V = 3072
 Q_COL = N
 V_COL = N + NQ
 
@@ -45,37 +45,36 @@ def tile_attend_pkv8q_silu_kernel(
         offs_t = sb.tile([P, N // 16], U16, name="offs_t")
         voffs_t = sb.tile([P, PAGES * DV // 16], U16, name="voffs_t")
         kw_pool = sb.tile([P, T], I32, name="kw_pool", align_bytes=64)
-        ks_pool = sb.tile([P, T], U8, name="ks_pool", align_bytes=64)
+        ks_pool = sb.tile([P, T], U8, name="ks_pool", tag="ks_then_vsc", align_bytes=64)
         vs_pool = sb.tile([P, T], F32, name="vs_pool", align_bytes=64)
-        vsc_pool = sb.tile([P, POOL_PAGES * DV], U8, name="vsc_pool", align_bytes=64)
+        vsc_pool = sb.tile([P, POOL_PAGES * DV], U8, name="vsc_pool", tag="vsc_then_vs", align_bytes=64)
         vw_pool = sb.tile([P, POOL_PAGES * DV], I32, name="vw_pool", align_bytes=64)
         qw = sb.tile([P, NQ], I32, name="qw", align_bytes=64)
         planes = sb.tile([P, V_COL + PAGES * DV], U8, name="planes", align_bytes=64)
 
-        nc.vector.memset(ks_pool[:].bitcast(I32), 0)
         nc.vector.memset(vsc_pool[:].bitcast(I32), 0)
+        nc.vector.memset(ks_pool[:].bitcast(I32), 0)
         nc.vector.memset(planes[:, Q_COL:V_COL].bitcast(I32), 0)
-        nc.vector.memset(vs_pool[0:VS_ROW, :].bitcast(I32), 0)
+        nc.vector.memset(vs_pool[0:VS_ROW, 0:FILL_V].bitcast(I32), 0)
+        nc.gpsimd.memset(vs_pool[0:VS_ROW, FILL_V - 8 : T].bitcast(I32), 0)
 
-        kw_hbm = k_words[0].rearrange("p n t -> p (n t)").bitcast(I32)
-        nc.sync.dma_start(kw_pool[:, 0:HEAD], kw_hbm[:, 0:HEAD])
+        nc.sync.dma_start(vs_pool[VS_ROW:P, :], vs[0:1, :])
         nc.sync.dma_start(offs_t[:], offs)
         nc.sync.dma_start(voffs_t[:], voffs)
-        nc.sync.dma_start(ks_pool[0:P:SPREAD, :].bitcast(I32), k_scales[0].bitcast(I32))
+        nc.sync.dma_start(qw[:], q_words[0, 0].rearrange("p n t -> p (n t)").bitcast(I32))
         nc.sync.dma_start(
             vsc_pool[0:P:SPREAD, :].bitcast(I32).rearrange("r (u e) -> r u e", u=POOL_PAGES),
             v_scales.bitcast(I32).rearrange("u r e -> r u e"),
         )
+        nc.sync.dma_start(ks_pool[0:P:SPREAD, :].bitcast(I32), k_scales[0].bitcast(I32))
         nc.sync.dma_start(planes[0:P:SPREAD, Q_COL:V_COL].bitcast(I32), q_scales[0, 0].bitcast(I32))
-        nc.sync.dma_start(vs_pool[VS_ROW:P, :], vs[0:1, :])
-        nc.sync.dma_start(kw_pool[:, HEAD:T], kw_hbm[:, HEAD:T])
-        nc.sync.dma_start(qw[:], q_words[0, 0].rearrange("p n t -> p (n t)").bitcast(I32))
+        nc.sync.dma_start(kw_pool[:], k_words[0].rearrange("p n t -> p (n t)").bitcast(I32))
         vw_sb = vw_pool[:].rearrange("p (u e) -> p u e", u=POOL_PAGES)
         vw_hbm = v_words.rearrange("u p e t -> p u (e t)").bitcast(I32)
         nc.sync.dma_start(vw_sb[:, 0:V_EARLY, :], vw_hbm[:, 0:V_EARLY, :])
 
-        ks_g = sb.tile([P, N], U8, name="ks_g", tag="gathered", align_bytes=64)
-        vsc_g = sb.tile([P, PAGES * DV], U8, name="vsc_g", align_bytes=64)
+        ks_g = sb.tile([P, N], U8, name="ks_g", align_bytes=64)
+        vsc_g = sb.tile([P, PAGES * DV], U8, name="vsc_g", tag="ks_then_vsc", align_bytes=64)
         vs_t = [sb.tile([P, PACK], F32, name=f"vs_t{g}", align_bytes=64) for g in range(PAGES)]
 
         def page_offs(g):
@@ -91,7 +90,7 @@ def tile_attend_pkv8q_silu_kernel(
         for r in range(1, 4):
             nc.sync.dma_start(planes[r:P:32, :].bitcast(I32), planes[SPREAD * r : P : 32, :].bitcast(I32))
         nc.sync.dma_start(vw_sb[:, V_EARLY:, :], vw_hbm[:, V_EARLY:, :])
-        vs_g = sb.tile([P, N], F32, name="vs_g", tag="gathered", align_bytes=64)
+        vs_g = sb.tile([P, N], F32, name="vs_g", tag="vsc_then_vs", align_bytes=64)
         for g in range(PAGES):
             page = slice(g * PAGE, (g + 1) * PAGE)
             nc.vector.tensor_copy(vs_g[:, page], vs_pool[:].indirect(page_offs(g)))

@@ -1,6 +1,7 @@
 from contextlib import ExitStack
 
 import concourse.mybir as mybir
+from concourse.masks import make_identity
 
 P = 128
 T = 4096
@@ -15,7 +16,6 @@ PACK = 4
 HALF = NQ // 2
 VS_ROW = P - 1
 SPREAD = 8
-V_EARLY = 3
 FILL_V = 3072
 Q_COL = N
 V_COL = N + NQ
@@ -40,42 +40,43 @@ def tile_attend_pkv8q_silu_kernel(
     nc = tc.nc
     with ExitStack() as ctx:
         sb = ctx.enter_context(tc.tile_pool(name="sb", bufs=1))
+        late = ctx.enter_context(tc.tile_pool(name="late", bufs=1))
         ps = ctx.enter_context(tc.psum_pool(name="ps", bufs=1))
 
         offs_t = sb.tile([P, N // 16], U16, name="offs_t")
         voffs_t = sb.tile([P, PAGES * DV // 16], U16, name="voffs_t")
         kw_pool = sb.tile([P, T], I32, name="kw_pool", align_bytes=64)
-        ks_pool = sb.tile([P, T], U8, name="ks_pool", tag="ks_then_vsc", align_bytes=64)
+        ks_pool = sb.tile([P, T], U8, name="ks_pool", align_bytes=64)
         vs_pool = sb.tile([P, T], F32, name="vs_pool", align_bytes=64)
         vsc_pool = sb.tile([P, POOL_PAGES * DV], U8, name="vsc_pool", tag="vsc_then_vs", align_bytes=64)
         vw_pool = sb.tile([P, POOL_PAGES * DV], I32, name="vw_pool", align_bytes=64)
         qw = sb.tile([P, NQ], I32, name="qw", align_bytes=64)
         planes = sb.tile([P, V_COL + PAGES * DV], U8, name="planes", align_bytes=64)
 
-        nc.vector.memset(vsc_pool[:].bitcast(I32), 0)
-        nc.vector.memset(ks_pool[:].bitcast(I32), 0)
+        ident = late.tile([P, P + 1], F32, name="ident", offset=768, align_bytes=64)
+
         nc.vector.memset(planes[:, Q_COL:V_COL].bitcast(I32), 0)
+        nc.vector.memset(ks_pool[:].bitcast(I32), 0)
+        nc.vector.memset(vsc_pool[:].bitcast(I32), 0)
         nc.vector.memset(vs_pool[0:VS_ROW, 0:FILL_V].bitcast(I32), 0)
+        nc.vector.memset(ident[:], 0.0)
         nc.gpsimd.memset(vs_pool[0:VS_ROW, FILL_V - 8 : T].bitcast(I32), 0)
+        make_identity(nc, ident[:, 0:P], nomemset=True)
 
         nc.sync.dma_start(vs_pool[VS_ROW:P, :], vs[0:1, :])
         nc.sync.dma_start(offs_t[:], offs)
         nc.sync.dma_start(voffs_t[:], voffs)
-        nc.sync.dma_start(qw[:], q_words[0, 0].rearrange("p n t -> p (n t)").bitcast(I32))
+        nc.sync.dma_start(planes[0:P:SPREAD, Q_COL:V_COL].bitcast(I32), q_scales[0, 0].bitcast(I32))
+        nc.sync.dma_start(ks_pool[0:P:SPREAD, :].bitcast(I32), k_scales[0].bitcast(I32))
         nc.sync.dma_start(
             vsc_pool[0:P:SPREAD, :].bitcast(I32).rearrange("r (u e) -> r u e", u=POOL_PAGES),
             v_scales.bitcast(I32).rearrange("u r e -> r u e"),
         )
-        nc.sync.dma_start(ks_pool[0:P:SPREAD, :].bitcast(I32), k_scales[0].bitcast(I32))
-        nc.sync.dma_start(planes[0:P:SPREAD, Q_COL:V_COL].bitcast(I32), q_scales[0, 0].bitcast(I32))
         nc.sync.dma_start(kw_pool[:], k_words[0].rearrange("p n t -> p (n t)").bitcast(I32))
-        vw_sb = vw_pool[:].rearrange("p (u e) -> p u e", u=POOL_PAGES)
-        vw_hbm = v_words.rearrange("u p e t -> p u (e t)").bitcast(I32)
-        nc.sync.dma_start(vw_sb[:, 0:V_EARLY, :], vw_hbm[:, 0:V_EARLY, :])
+        nc.sync.dma_start(qw[:], q_words[0, 0].rearrange("p n t -> p (n t)").bitcast(I32))
 
         ks_g = sb.tile([P, N], U8, name="ks_g", align_bytes=64)
-        vsc_g = sb.tile([P, PAGES * DV], U8, name="vsc_g", tag="ks_then_vsc", align_bytes=64)
-        vs_t = [sb.tile([P, PACK], F32, name=f"vs_t{g}", align_bytes=64) for g in range(PAGES)]
+        vsc_g = sb.tile([P, PAGES * DV], U8, name="vsc_g", align_bytes=64)
 
         def page_offs(g):
             return offs_t[:, g * (PAGE // 16) : (g + 1) * (PAGE // 16)]
@@ -89,12 +90,17 @@ def tile_attend_pkv8q_silu_kernel(
         nc.vector.tensor_copy(planes[:, V_COL:].bitcast(I32), vsc_g[:].bitcast(I32))
         for r in range(1, 4):
             nc.sync.dma_start(planes[r:P:32, :].bitcast(I32), planes[SPREAD * r : P : 32, :].bitcast(I32))
-        nc.sync.dma_start(vw_sb[:, V_EARLY:, :], vw_hbm[:, V_EARLY:, :])
+        nc.sync.dma_start(
+            vw_pool[:].rearrange("p (u e) -> p u e", u=POOL_PAGES),
+            v_words.rearrange("u p e t -> p u (e t)").bitcast(I32),
+        )
         vs_g = sb.tile([P, N], F32, name="vs_g", tag="vsc_then_vs", align_bytes=64)
+        vs_t = [ps.tile([P, PACK, P], F32, name=f"vs_t{g}") for g in range(PAGES)]
         for g in range(PAGES):
             page = slice(g * PAGE, (g + 1) * PAGE)
             nc.vector.tensor_copy(vs_g[:, page], vs_pool[:].indirect(page_offs(g)))
-            nc.sync.dma_start(vs_t[g][:], vs_g[VS_ROW:P, page].rearrange("p (s t) -> p s t", t=PACK))
+            for t in range(PACK):
+                nc.tensor.transpose(vs_t[g][:, t, :], vs_g[:, g * PAGE + t : (g + 1) * PAGE : PACK], ident[:, 0:P])
 
         kw_g = sb.tile([P, N], U32, name="kw_g", align_bytes=64)
         score = [ps.tile([P, PACK, NQ], F32, name=f"score{g}") for g in range(PAGES)]
@@ -115,20 +121,17 @@ def tile_attend_pkv8q_silu_kernel(
                     stop=True,
                 )
 
-        vw_g = sb.tile([P, PAGES * DV], U32, name="vw_g", align_bytes=64)
-        nc.vector.tensor_copy(vw_g[:], vw_pool[:].bitcast(U32).indirect(voffs_t[:]))
-
         w16 = [sb.tile([P, NQ, PACK], BF16, name=f"w16_{g}", align_bytes=64) for g in range(PAGES)]
         wsc = [sb.tile([P, NQ], U8, name=f"wsc{g}", align_bytes=64) for g in range(PAGES)]
 
-        def weigh(g, h):
+        def weigh(g, h, bias):
             cols = slice(h * HALF, (h + 1) * HALF)
             p32 = sb.tile([P, HALF, PACK], F32, name=f"p32_{g}{h}", tag=f"p32_{g}{h}", align_bytes=64)
-            nc.scalar.activation(p32[:], score[g][:, :, cols].rearrange("p t q -> p q t"), SILU)
+            nc.scalar.activation(p32[:], score[g][:, :, cols].rearrange("p t q -> p q t"), SILU, bias=bias)
             nc.vector.tensor_tensor(
                 w16[g][:, cols, :],
                 p32[:],
-                vs_t[g][:].unsqueeze(1).to_broadcast([P, HALF, PACK]),
+                vs_t[g][:, :, VS_ROW].unsqueeze(1).to_broadcast([P, HALF, PACK]),
                 MULT,
             )
 
@@ -141,9 +144,11 @@ def tile_attend_pkv8q_silu_kernel(
 
         for g in range(PAGES):
             for h in range(2):
-                weigh(g, h)
+                weigh(g, h, ident[:, P : P + 1] if (g, h) == (PAGES - 1, 1) else 0.0)
+        vw_g = late.tile([P, PAGES * DV], U32, name="vw_g", offset=0, align_bytes=64)
+        nc.vector.tensor_copy(vw_g[:], vw_pool[:].bitcast(U32).indirect(voffs_t[:]))
         wq = [
-            sb.tile([P, NQ], U32, name="wq0", tag="p32_10", align_bytes=64),
+            late.tile([P, NQ], U32, name="wq0", offset=1024, align_bytes=64),
             sb.tile([P, NQ], U32, name="wq1", align_bytes=64),
         ]
         quantize(0, slice(0, NQ))

@@ -1,7 +1,6 @@
 from contextlib import ExitStack
 
 import concourse.mybir as mybir
-from concourse.masks import make_identity
 
 P = 128
 T = 4096
@@ -16,7 +15,8 @@ PACK = 4
 HALF = NQ // 2
 VS_ROW = P - 1
 SPREAD = 8
-FILL_V = 3072
+FILL_V = 2880
+V_FIRST = 4
 Q_COL = N
 V_COL = N + NQ
 
@@ -53,15 +53,14 @@ def tile_attend_pkv8q_silu_kernel(
         qw = sb.tile([P, NQ], I32, name="qw", align_bytes=64)
         planes = sb.tile([P, V_COL + PAGES * DV], U8, name="planes", align_bytes=64)
 
-        ident = late.tile([P, P + 1], F32, name="ident", offset=768, align_bytes=64)
+        zero = late.tile([P, 32], F32, name="zero", offset=960, align_bytes=64)
 
         nc.vector.memset(planes[:, Q_COL:V_COL].bitcast(I32), 0)
         nc.vector.memset(ks_pool[:].bitcast(I32), 0)
         nc.vector.memset(vsc_pool[:].bitcast(I32), 0)
         nc.vector.memset(vs_pool[0:VS_ROW, 0:FILL_V].bitcast(I32), 0)
-        nc.vector.memset(ident[:], 0.0)
+        nc.vector.memset(zero[:, 0:1], 0.0)
         nc.gpsimd.memset(vs_pool[0:VS_ROW, FILL_V - 8 : T].bitcast(I32), 0)
-        make_identity(nc, ident[:, 0:P], nomemset=True)
 
         nc.sync.dma_start(vs_pool[VS_ROW:P, :], vs[0:1, :])
         nc.sync.dma_start(offs_t[:], offs)
@@ -90,17 +89,16 @@ def tile_attend_pkv8q_silu_kernel(
         nc.vector.tensor_copy(planes[:, V_COL:].bitcast(I32), vsc_g[:].bitcast(I32))
         for r in range(1, 4):
             nc.sync.dma_start(planes[r:P:32, :].bitcast(I32), planes[SPREAD * r : P : 32, :].bitcast(I32))
-        nc.sync.dma_start(
-            vw_pool[:].rearrange("p (u e) -> p u e", u=POOL_PAGES),
-            v_words.rearrange("u p e t -> p u (e t)").bitcast(I32),
-        )
+        vw_sb = vw_pool[:].rearrange("p (u e) -> p u e", u=POOL_PAGES)
+        vw_hbm = v_words.rearrange("u p e t -> p u (e t)").bitcast(I32)
+        nc.sync.dma_start(vw_sb[:, 0:V_FIRST, :], vw_hbm[:, 0:V_FIRST, :])
         vs_g = sb.tile([P, N], F32, name="vs_g", tag="vsc_then_vs", align_bytes=64)
-        vs_t = [ps.tile([P, PACK, P], F32, name=f"vs_t{g}") for g in range(PAGES)]
+        vs_t = [sb.tile([P, PACK], F32, name=f"vs_t{g}", align_bytes=64) for g in range(PAGES)]
         for g in range(PAGES):
             page = slice(g * PAGE, (g + 1) * PAGE)
             nc.vector.tensor_copy(vs_g[:, page], vs_pool[:].indirect(page_offs(g)))
-            for t in range(PACK):
-                nc.tensor.transpose(vs_t[g][:, t, :], vs_g[:, g * PAGE + t : (g + 1) * PAGE : PACK], ident[:, 0:P])
+            nc.sync.dma_start(vs_t[g][:], vs_g[VS_ROW:P, page].rearrange("p (s t) -> p s t", t=PACK))
+        nc.sync.dma_start(vw_sb[:, V_FIRST:, :], vw_hbm[:, V_FIRST:, :])
 
         kw_g = sb.tile([P, N], U32, name="kw_g", align_bytes=64)
         score = [ps.tile([P, PACK, NQ], F32, name=f"score{g}") for g in range(PAGES)]
@@ -131,7 +129,7 @@ def tile_attend_pkv8q_silu_kernel(
             nc.vector.tensor_tensor(
                 w16[g][:, cols, :],
                 p32[:],
-                vs_t[g][:, :, VS_ROW].unsqueeze(1).to_broadcast([P, HALF, PACK]),
+                vs_t[g][:].unsqueeze(1).to_broadcast([P, HALF, PACK]),
                 MULT,
             )
 
@@ -144,7 +142,7 @@ def tile_attend_pkv8q_silu_kernel(
 
         for g in range(PAGES):
             for h in range(2):
-                weigh(g, h, ident[:, P : P + 1] if (g, h) == (PAGES - 1, 1) else 0.0)
+                weigh(g, h, zero[:, 0:1] if (g, h) == (PAGES - 1, 1) else 0.0)
         vw_g = late.tile([P, PAGES * DV], U32, name="vw_g", offset=0, align_bytes=64)
         nc.vector.tensor_copy(vw_g[:], vw_pool[:].bitcast(U32).indirect(voffs_t[:]))
         wq = [

@@ -16,7 +16,8 @@ HALF = NQ // 2
 VS_ROW = P - 1
 SPREAD = 8
 FILL_V = 2880
-V_FIRST = 4
+V_FIRST = 2
+K_FIRST = 640
 Q_COL = N
 V_COL = N + NQ
 
@@ -40,7 +41,6 @@ def tile_attend_pkv8q_silu_kernel(
     nc = tc.nc
     with ExitStack() as ctx:
         sb = ctx.enter_context(tc.tile_pool(name="sb", bufs=1))
-        late = ctx.enter_context(tc.tile_pool(name="late", bufs=1))
         ps = ctx.enter_context(tc.psum_pool(name="ps", bufs=1))
 
         offs_t = sb.tile([P, N // 16], U16, name="offs_t")
@@ -53,16 +53,14 @@ def tile_attend_pkv8q_silu_kernel(
         qw = sb.tile([P, NQ], I32, name="qw", align_bytes=64)
         planes = sb.tile([P, V_COL + PAGES * DV], U8, name="planes", align_bytes=64)
 
-        zero = late.tile([P, 32], F32, name="zero", offset=960, align_bytes=64)
-
         nc.vector.memset(planes[:, Q_COL:V_COL].bitcast(I32), 0)
         nc.vector.memset(ks_pool[:].bitcast(I32), 0)
         nc.vector.memset(vsc_pool[:].bitcast(I32), 0)
         nc.vector.memset(vs_pool[0:VS_ROW, 0:FILL_V].bitcast(I32), 0)
-        nc.vector.memset(zero[:, 0:1], 0.0)
         nc.gpsimd.memset(vs_pool[0:VS_ROW, FILL_V - 8 : T].bitcast(I32), 0)
 
-        nc.sync.dma_start(vs_pool[VS_ROW:P, :], vs[0:1, :])
+        kw_hbm = k_words[0].rearrange("p n t -> p (n t)").bitcast(I32)
+        nc.sync.dma_start(kw_pool[:, 0:K_FIRST], kw_hbm[:, 0:K_FIRST])
         nc.sync.dma_start(offs_t[:], offs)
         nc.sync.dma_start(voffs_t[:], voffs)
         nc.sync.dma_start(planes[0:P:SPREAD, Q_COL:V_COL].bitcast(I32), q_scales[0, 0].bitcast(I32))
@@ -71,8 +69,12 @@ def tile_attend_pkv8q_silu_kernel(
             vsc_pool[0:P:SPREAD, :].bitcast(I32).rearrange("r (u e) -> r u e", u=POOL_PAGES),
             v_scales.bitcast(I32).rearrange("u r e -> r u e"),
         )
-        nc.sync.dma_start(kw_pool[:], k_words[0].rearrange("p n t -> p (n t)").bitcast(I32))
+        nc.sync.dma_start(vs_pool[VS_ROW:P, :], vs[0:1, :])
+        nc.sync.dma_start(kw_pool[:, K_FIRST:], kw_hbm[:, K_FIRST:])
         nc.sync.dma_start(qw[:], q_words[0, 0].rearrange("p n t -> p (n t)").bitcast(I32))
+        vw_sb = vw_pool[:].rearrange("p (u e) -> p u e", u=POOL_PAGES)
+        vw_hbm = v_words.rearrange("u p e t -> p u (e t)").bitcast(I32)
+        nc.sync.dma_start(vw_sb[:, 0:V_FIRST, :], vw_hbm[:, 0:V_FIRST, :])
 
         ks_g = sb.tile([P, N], U8, name="ks_g", align_bytes=64)
         vsc_g = sb.tile([P, PAGES * DV], U8, name="vsc_g", align_bytes=64)
@@ -89,16 +91,13 @@ def tile_attend_pkv8q_silu_kernel(
         nc.vector.tensor_copy(planes[:, V_COL:].bitcast(I32), vsc_g[:].bitcast(I32))
         for r in range(1, 4):
             nc.sync.dma_start(planes[r:P:32, :].bitcast(I32), planes[SPREAD * r : P : 32, :].bitcast(I32))
-        vw_sb = vw_pool[:].rearrange("p (u e) -> p u e", u=POOL_PAGES)
-        vw_hbm = v_words.rearrange("u p e t -> p u (e t)").bitcast(I32)
-        nc.sync.dma_start(vw_sb[:, 0:V_FIRST, :], vw_hbm[:, 0:V_FIRST, :])
+        nc.sync.dma_start(vw_sb[:, V_FIRST:, :], vw_hbm[:, V_FIRST:, :])
         vs_g = sb.tile([P, N], F32, name="vs_g", tag="vsc_then_vs", align_bytes=64)
         vs_t = [sb.tile([P, PACK], F32, name=f"vs_t{g}", align_bytes=64) for g in range(PAGES)]
         for g in range(PAGES):
             page = slice(g * PAGE, (g + 1) * PAGE)
             nc.vector.tensor_copy(vs_g[:, page], vs_pool[:].indirect(page_offs(g)))
             nc.sync.dma_start(vs_t[g][:], vs_g[VS_ROW:P, page].rearrange("p (s t) -> p s t", t=PACK))
-        nc.sync.dma_start(vw_sb[:, V_FIRST:, :], vw_hbm[:, V_FIRST:, :])
 
         kw_g = sb.tile([P, N], U32, name="kw_g", align_bytes=64)
         score = [ps.tile([P, PACK, NQ], F32, name=f"score{g}") for g in range(PAGES)]
@@ -119,13 +118,16 @@ def tile_attend_pkv8q_silu_kernel(
                     stop=True,
                 )
 
+        vw_g = sb.tile([P, PAGES * DV], U32, name="vw_g", align_bytes=64)
+        nc.vector.tensor_copy(vw_g[:], vw_pool[:].bitcast(U32).indirect(voffs_t[:]))
+
         w16 = [sb.tile([P, NQ, PACK], BF16, name=f"w16_{g}", align_bytes=64) for g in range(PAGES)]
         wsc = [sb.tile([P, NQ], U8, name=f"wsc{g}", align_bytes=64) for g in range(PAGES)]
 
-        def weigh(g, h, bias):
+        def weigh(g, h):
             cols = slice(h * HALF, (h + 1) * HALF)
             p32 = sb.tile([P, HALF, PACK], F32, name=f"p32_{g}{h}", tag=f"p32_{g}{h}", align_bytes=64)
-            nc.scalar.activation(p32[:], score[g][:, :, cols].rearrange("p t q -> p q t"), SILU, bias=bias)
+            nc.scalar.activation(p32[:], score[g][:, :, cols].rearrange("p t q -> p q t"), SILU)
             nc.vector.tensor_tensor(
                 w16[g][:, cols, :],
                 p32[:],
@@ -142,11 +144,9 @@ def tile_attend_pkv8q_silu_kernel(
 
         for g in range(PAGES):
             for h in range(2):
-                weigh(g, h, zero[:, 0:1] if (g, h) == (PAGES - 1, 1) else 0.0)
-        vw_g = late.tile([P, PAGES * DV], U32, name="vw_g", offset=0, align_bytes=64)
-        nc.vector.tensor_copy(vw_g[:], vw_pool[:].bitcast(U32).indirect(voffs_t[:]))
+                weigh(g, h)
         wq = [
-            late.tile([P, NQ], U32, name="wq0", offset=1024, align_bytes=64),
+            sb.tile([P, NQ], U32, name="wq0", tag="p32_10", align_bytes=64),
             sb.tile([P, NQ], U32, name="wq1", align_bytes=64),
         ]
         quantize(0, slice(0, NQ))

@@ -16,7 +16,7 @@ HALF = NQ // 2
 VS_ROW = P - 1
 SPREAD = 8
 FILL_V = 2880
-V_FIRST = 2
+V_FIRST = 4
 K_FIRST = 640
 Q_COL = N
 V_COL = N + NQ

@@ -15,9 +15,8 @@ PACK = 4
 HALF = NQ // 2
 VS_ROW = P - 1
 SPREAD = 8
-FILL_V = 2880
-V_FIRST = 4
-K_FIRST = 640
+FILL_V = 2048
+V_FIRST = 2
 Q_COL = N
 V_COL = N + NQ
 
@@ -57,10 +56,10 @@ def tile_attend_pkv8q_silu_kernel(
         nc.vector.memset(ks_pool[:].bitcast(I32), 0)
         nc.vector.memset(vsc_pool[:].bitcast(I32), 0)
         nc.vector.memset(vs_pool[0:VS_ROW, 0:FILL_V].bitcast(I32), 0)
-        nc.gpsimd.memset(vs_pool[0:VS_ROW, FILL_V - 8 : T].bitcast(I32), 0)
 
-        kw_hbm = k_words[0].rearrange("p n t -> p (n t)").bitcast(I32)
-        nc.sync.dma_start(kw_pool[:, 0:K_FIRST], kw_hbm[:, 0:K_FIRST])
+        vs_head = sb.tile([P, 8], F32, name="vs_head", align_bytes=64)
+        nc.sync.dma_start(vs_head[:], vs[:, 0:8])
+        nc.sync.dma_start(vs_pool[VS_ROW:P, :], vs[0:1, :])
         nc.sync.dma_start(offs_t[:], offs)
         nc.sync.dma_start(voffs_t[:], voffs)
         nc.sync.dma_start(planes[0:P:SPREAD, Q_COL:V_COL].bitcast(I32), q_scales[0, 0].bitcast(I32))
@@ -69,13 +68,15 @@ def tile_attend_pkv8q_silu_kernel(
             vsc_pool[0:P:SPREAD, :].bitcast(I32).rearrange("r (u e) -> r u e", u=POOL_PAGES),
             v_scales.bitcast(I32).rearrange("u r e -> r u e"),
         )
-        nc.sync.dma_start(vs_pool[VS_ROW:P, :], vs[0:1, :])
-        nc.sync.dma_start(kw_pool[:, K_FIRST:], kw_hbm[:, K_FIRST:])
+        nc.sync.dma_start(kw_pool[:], k_words[0].rearrange("p n t -> p (n t)").bitcast(I32))
         nc.sync.dma_start(qw[:], q_words[0, 0].rearrange("p n t -> p (n t)").bitcast(I32))
         vw_sb = vw_pool[:].rearrange("p (u e) -> p u e", u=POOL_PAGES)
         vw_hbm = v_words.rearrange("u p e t -> p u (e t)").bitcast(I32)
         nc.sync.dma_start(vw_sb[:, 0:V_FIRST, :], vw_hbm[:, 0:V_FIRST, :])
 
+        nc.scalar.activation(
+            vs_pool[0:VS_ROW, FILL_V:T], vs_head[0:VS_ROW, 0:1].to_broadcast([VS_ROW, T - FILL_V]), COPY
+        )
         ks_g = sb.tile([P, N], U8, name="ks_g", align_bytes=64)
         vsc_g = sb.tile([P, PAGES * DV], U8, name="vsc_g", align_bytes=64)
 
@@ -93,11 +94,15 @@ def tile_attend_pkv8q_silu_kernel(
             nc.sync.dma_start(planes[r:P:32, :].bitcast(I32), planes[SPREAD * r : P : 32, :].bitcast(I32))
         nc.sync.dma_start(vw_sb[:, V_FIRST:, :], vw_hbm[:, V_FIRST:, :])
         vs_g = sb.tile([P, N], F32, name="vs_g", tag="vsc_then_vs", align_bytes=64)
-        vs_t = [sb.tile([P, PACK], F32, name=f"vs_t{g}", align_bytes=64) for g in range(PAGES)]
-        for g in range(PAGES):
-            page = slice(g * PAGE, (g + 1) * PAGE)
-            nc.vector.tensor_copy(vs_g[:, page], vs_pool[:].indirect(page_offs(g)))
-            nc.sync.dma_start(vs_t[g][:], vs_g[VS_ROW:P, page].rearrange("p (s t) -> p s t", t=PACK))
+        vs_t = sb.tile([P, PAGES, PACK], F32, name="vs_t", align_bytes=64)
+        nc.vector.tensor_copy(
+            vs_g[:].bitcast(U32).rearrange("p (s g t) -> p g s t", g=PAGES, t=PACK),
+            vs_pool[:].bitcast(U32).indirect(offs_t[:]),
+        )
+        nc.sync.dma_start(
+            vs_t[:].rearrange("p g t -> p (g t)"),
+            vs_g[VS_ROW:P, :].rearrange("p (s c) -> p s c", c=PAGES * PACK),
+        )
 
         kw_g = sb.tile([P, N], U32, name="kw_g", align_bytes=64)
         score = [ps.tile([P, PACK, NQ], F32, name=f"score{g}") for g in range(PAGES)]
@@ -131,7 +136,7 @@ def tile_attend_pkv8q_silu_kernel(
             nc.vector.tensor_tensor(
                 w16[g][:, cols, :],
                 p32[:],
-                vs_t[g][:].unsqueeze(1).to_broadcast([P, HALF, PACK]),
+                vs_t[:, g, :].unsqueeze(1).to_broadcast([P, HALF, PACK]),
                 MULT,
             )
 

@@ -12,6 +12,7 @@ NQ = 128
 DV = 128
 D = 512
 PACK = 4
+PAIR = 2
 HALF = NQ // 2
 VS_ROW = P - 1
 SPREAD = 8
@@ -105,7 +106,9 @@ def tile_attend_pkv8q_silu_kernel(
         )
 
         kw_g = sb.tile([P, N], U32, name="kw_g", align_bytes=64)
-        score = [ps.tile([P, PACK, NQ], F32, name=f"score{g}") for g in range(PAGES)]
+        score = [
+            [ps.tile([P, PAIR, NQ], F32, name=f"score{g}{u}") for u in range(PACK // PAIR)] for g in range(PAGES)
+        ]
         for g in range(PAGES):
             nc.vector.tensor_copy(
                 kw_g[:, g * PAGE : (g + 1) * PAGE].rearrange("p (t s) -> p s t", t=PACK),
@@ -114,7 +117,7 @@ def tile_attend_pkv8q_silu_kernel(
             for t in range(PACK):
                 slots = slice(g * PAGE + t * P, g * PAGE + (t + 1) * P)
                 nc.tensor.matmul_mx(
-                    out=score[g][:, t, :],
+                    out=score[g][t // PAIR][:, t % PAIR, :],
                     lhsT=kw_g[:, slots].bitcast(FP8X4),
                     lhsT_scale=planes[:, slots],
                     rhs=qw[:].bitcast(FP8X4),
@@ -128,17 +131,29 @@ def tile_attend_pkv8q_silu_kernel(
 
         w16 = [sb.tile([P, NQ, PACK], BF16, name=f"w16_{g}", align_bytes=64) for g in range(PAGES)]
         wsc = [sb.tile([P, NQ], U8, name=f"wsc{g}", align_bytes=64) for g in range(PAGES)]
+        halves = [slice(0, HALF), slice(HALF, NQ)]
 
-        def weigh(g, h):
-            cols = slice(h * HALF, (h + 1) * HALF)
-            p32 = sb.tile([P, HALF, PACK], F32, name=f"p32_{g}{h}", tag=f"p32_{g}{h}", align_bytes=64)
-            nc.scalar.activation(p32[:], score[g][:, :, cols].rearrange("p t q -> p q t"), SILU)
-            nc.vector.tensor_tensor(
-                w16[g][:, cols, :],
-                p32[:],
-                vs_t[:, g, :].unsqueeze(1).to_broadcast([P, HALF, PACK]),
-                MULT,
-            )
+        for g in range(PAGES):
+            p32 = [
+                sb.tile([P, PACK // PAIR, HALF, PAIR], F32, name=f"p32_{g}{h}", tag=f"p32_{g}{h}", align_bytes=64)
+                for h in range(2)
+            ]
+            for u in range(PACK // PAIR):
+                for h, cols in enumerate(halves):
+                    nc.scalar.activation(p32[h][:, u, :, :], score[g][u][:, :, cols].rearrange("p t q -> p q t"), SILU)
+            for h, cols in enumerate(halves):
+                nc.vector.tensor_tensor(
+                    w16[g][:, cols, :].rearrange("p q (u t) -> p q u t", t=PAIR),
+                    p32[h][:].rearrange("p u q t -> p q u t"),
+                    vs_t[:, g, :].rearrange("p (u t) -> p u t", t=PAIR).unsqueeze(1).to_broadcast(
+                        [P, HALF, PACK // PAIR, PAIR]
+                    ),
+                    MULT,
+                )
+        wq = [
+            sb.tile([P, NQ], U32, name="wq0", tag="p32_10", align_bytes=64),
+            sb.tile([P, NQ], U32, name="wq1", align_bytes=64),
+        ]
 
         def quantize(g, cols):
             nc.vector.quantize_mx(
@@ -147,16 +162,9 @@ def tile_attend_pkv8q_silu_kernel(
                 in_=w16[g][:, cols, :].rearrange("p q t -> p (q t)"),
             )
 
-        for g in range(PAGES):
-            for h in range(2):
-                weigh(g, h)
-        wq = [
-            sb.tile([P, NQ], U32, name="wq0", tag="p32_10", align_bytes=64),
-            sb.tile([P, NQ], U32, name="wq1", align_bytes=64),
-        ]
         quantize(0, slice(0, NQ))
-        quantize(1, slice(0, HALF))
-        quantize(1, slice(HALF, NQ))
+        for cols in halves:
+            quantize(1, cols)
 
         acc = ps.tile([P, DV], F32, name="acc")
         for g in range(PAGES):

@@ -16,7 +16,7 @@ PAIR = 2
 HALF = NQ // 2
 VS_ROW = P - 1
 SPREAD = 8
-FILL_V = 2048
+FILL_V = 2688
 V_FIRST = 2
 Q_COL = N
 V_COL = N + NQ

@@ -16,8 +16,8 @@ PAIR = 2
 HALF = NQ // 2
 VS_ROW = P - 1
 SPREAD = 8
-FILL_V = 2688
-V_FIRST = 2
+K_FIRST = 256
+V_FIRST = 4
 Q_COL = N
 V_COL = N + NQ
 
@@ -48,38 +48,40 @@ def tile_attend_pkv8q_silu_kernel(
         kw_pool = sb.tile([P, T], I32, name="kw_pool", align_bytes=64)
         ks_pool = sb.tile([P, T], U8, name="ks_pool", align_bytes=64)
         vs_pool = sb.tile([P, T], F32, name="vs_pool", align_bytes=64)
-        vsc_pool = sb.tile([P, POOL_PAGES * DV], U8, name="vsc_pool", tag="vsc_then_vs", align_bytes=64)
+        vsc_pool = sb.tile([P, POOL_PAGES * DV], U8, name="vsc_pool", align_bytes=64)
         vw_pool = sb.tile([P, POOL_PAGES * DV], I32, name="vw_pool", align_bytes=64)
         qw = sb.tile([P, NQ], I32, name="qw", align_bytes=64)
         planes = sb.tile([P, V_COL + PAGES * DV], U8, name="planes", align_bytes=64)
 
-        nc.vector.memset(planes[:, Q_COL:V_COL].bitcast(I32), 0)
         nc.vector.memset(ks_pool[:].bitcast(I32), 0)
+        warm = sb.tile([P, 2], F32, name="warm", align_bytes=64)
+        nc.vector.memset(warm[:, 0:1], 0.0)
         nc.vector.memset(vsc_pool[:].bitcast(I32), 0)
-        nc.vector.memset(vs_pool[0:VS_ROW, 0:FILL_V].bitcast(I32), 0)
+        nc.vector.memset(planes[:, Q_COL:V_COL].bitcast(I32), 0)
+        nc.vector.memset(vs_pool[0:VS_ROW, :].bitcast(I32), 0)
+        nc.scalar.activation(warm[:, 1:2], warm[:, 0:1], SILU)
 
-        vs_head = sb.tile([P, 8], F32, name="vs_head", align_bytes=64)
-        nc.sync.dma_start(vs_head[:], vs[:, 0:8])
+        kw_hbm = k_words[0].rearrange("p n t -> p (n t)").bitcast(I32)
         nc.sync.dma_start(vs_pool[VS_ROW:P, :], vs[0:1, :])
+        nc.sync.dma_start(kw_pool[:, 0:K_FIRST], kw_hbm[:, 0:K_FIRST])
         nc.sync.dma_start(offs_t[:], offs)
         nc.sync.dma_start(voffs_t[:], voffs)
-        nc.sync.dma_start(planes[0:P:SPREAD, Q_COL:V_COL].bitcast(I32), q_scales[0, 0].bitcast(I32))
         nc.sync.dma_start(ks_pool[0:P:SPREAD, :].bitcast(I32), k_scales[0].bitcast(I32))
         nc.sync.dma_start(
             vsc_pool[0:P:SPREAD, :].bitcast(I32).rearrange("r (u e) -> r u e", u=POOL_PAGES),
             v_scales.bitcast(I32).rearrange("u r e -> r u e"),
         )
-        nc.sync.dma_start(kw_pool[:], k_words[0].rearrange("p n t -> p (n t)").bitcast(I32))
+        nc.sync.dma_start(planes[0:P:SPREAD, Q_COL:V_COL].bitcast(I32), q_scales[0, 0].bitcast(I32))
+        nc.sync.dma_start(kw_pool[:, K_FIRST:], kw_hbm[:, K_FIRST:])
         nc.sync.dma_start(qw[:], q_words[0, 0].rearrange("p n t -> p (n t)").bitcast(I32))
         vw_sb = vw_pool[:].rearrange("p (u e) -> p u e", u=POOL_PAGES)
         vw_hbm = v_words.rearrange("u p e t -> p u (e t)").bitcast(I32)
         nc.sync.dma_start(vw_sb[:, 0:V_FIRST, :], vw_hbm[:, 0:V_FIRST, :])
 
-        nc.scalar.activation(
-            vs_pool[0:VS_ROW, FILL_V:T], vs_head[0:VS_ROW, 0:1].to_broadcast([VS_ROW, T - FILL_V]), COPY
-        )
+        vs_n = sb.tile([P, N], F32, name="vs_n", align_bytes=64)
+        nc.scalar.activation(vs_n[:], vs_pool[:].indirect(offs_t[:]), COPY)
         ks_g = sb.tile([P, N], U8, name="ks_g", align_bytes=64)
-        vsc_g = sb.tile([P, PAGES * DV], U8, name="vsc_g", align_bytes=64)
+        vsc_g = sb.tile([P, PAGES * DV], U8, name="vsc_g", tag="vsc_then_vs", align_bytes=64)
 
         def page_offs(g):
             return offs_t[:, g * (PAGE // 16) : (g + 1) * (PAGE // 16)]
@@ -97,8 +99,8 @@ def tile_attend_pkv8q_silu_kernel(
         vs_g = sb.tile([P, N], F32, name="vs_g", tag="vsc_then_vs", align_bytes=64)
         vs_t = sb.tile([P, PAGES, PACK], F32, name="vs_t", align_bytes=64)
         nc.vector.tensor_copy(
-            vs_g[:].bitcast(U32).rearrange("p (s g t) -> p g s t", g=PAGES, t=PACK),
-            vs_pool[:].bitcast(U32).indirect(offs_t[:]),
+            vs_g[96:P, :].rearrange("p (s g t) -> p s g t", g=PAGES, t=PACK),
+            vs_n[96:P, :].rearrange("p (g s t) -> p s g t", g=PAGES, t=PACK),
         )
         nc.sync.dma_start(
             vs_t[:].rearrange("p g t -> p (g t)"),
@@ -134,24 +136,23 @@ def tile_attend_pkv8q_silu_kernel(
         halves = [slice(0, HALF), slice(HALF, NQ)]
 
         for g in range(PAGES):
-            p32 = [
-                sb.tile([P, PACK // PAIR, HALF, PAIR], F32, name=f"p32_{g}{h}", tag=f"p32_{g}{h}", align_bytes=64)
-                for h in range(2)
-            ]
-            for u in range(PACK // PAIR):
-                for h, cols in enumerate(halves):
-                    nc.scalar.activation(p32[h][:, u, :, :], score[g][u][:, :, cols].rearrange("p t q -> p q t"), SILU)
+            p32 = sb.tile([P, 2, PACK // PAIR, HALF, PAIR], F32, name=f"p32_{g}", align_bytes=64)
+            nc.scalar.activation(
+                p32[:, :, 0, :, :], score[g][0][:].rearrange("p t (h q) -> p h q t", h=2), SILU
+            )
+            for h, cols in enumerate(halves):
+                nc.scalar.activation(p32[:, h, 1, :, :], score[g][1][:, :, cols].rearrange("p t q -> p q t"), SILU)
             for h, cols in enumerate(halves):
                 nc.vector.tensor_tensor(
                     w16[g][:, cols, :].rearrange("p q (u t) -> p q u t", t=PAIR),
-                    p32[h][:].rearrange("p u q t -> p q u t"),
+                    p32[:, h].rearrange("p u q t -> p q u t"),
                     vs_t[:, g, :].rearrange("p (u t) -> p u t", t=PAIR).unsqueeze(1).to_broadcast(
                         [P, HALF, PACK // PAIR, PAIR]
                     ),
                     MULT,
                 )
         wq = [
-            sb.tile([P, NQ], U32, name="wq0", tag="p32_10", align_bytes=64),
+            sb.tile([P, NQ], U32, name="wq0", align_bytes=64),
             sb.tile([P, NQ], U32, name="wq1", align_bytes=64),
         ]
 

@@ -78,8 +78,6 @@ def tile_attend_pkv8q_silu_kernel(
         vw_hbm = v_words.rearrange("u p e t -> p u (e t)").bitcast(I32)
         nc.sync.dma_start(vw_sb[:, 0:V_FIRST, :], vw_hbm[:, 0:V_FIRST, :])
 
-        vs_n = sb.tile([P, N], F32, name="vs_n", align_bytes=64)
-        nc.scalar.activation(vs_n[:], vs_pool[:].indirect(offs_t[:]), COPY)
         ks_g = sb.tile([P, N], U8, name="ks_g", align_bytes=64)
         vsc_g = sb.tile([P, PAGES * DV], U8, name="vsc_g", tag="vsc_then_vs", align_bytes=64)
 
@@ -98,10 +96,11 @@ def tile_attend_pkv8q_silu_kernel(
         nc.sync.dma_start(vw_sb[:, V_FIRST:, :], vw_hbm[:, V_FIRST:, :])
         vs_g = sb.tile([P, N], F32, name="vs_g", tag="vsc_then_vs", align_bytes=64)
         vs_t = sb.tile([P, PAGES, PACK], F32, name="vs_t", align_bytes=64)
-        nc.vector.tensor_copy(
-            vs_g[96:P, :].rearrange("p (s g t) -> p s g t", g=PAGES, t=PACK),
-            vs_n[96:P, :].rearrange("p (g s t) -> p s g t", g=PAGES, t=PACK),
-        )
+        vs_by_page = vs_g[:].rearrange("p (s g t) -> p g s t", g=PAGES, t=PACK)
+        vs_first = sb.tile([P, PAGE], F32, name="vs_first", align_bytes=64)
+        nc.scalar.activation(vs_first[:], vs_pool[:].indirect(page_offs(0)), COPY)
+        nc.scalar.activation(vs_by_page[:, 0], vs_first[:].rearrange("p (s t) -> p s t", t=PACK), COPY)
+        nc.vector.tensor_copy(vs_by_page[:, 1].bitcast(U32), vs_pool[:].bitcast(U32).indirect(page_offs(1)))
         nc.sync.dma_start(
             vs_t[:].rearrange("p g t -> p (g t)"),
             vs_g[VS_ROW:P, :].rearrange("p (s c) -> p s c", c=PAGES * PACK),

@@ -17,7 +17,9 @@ HALF = NQ // 2
 VS_ROW = P - 1
 SPREAD = 8
 K_FIRST = 256
-V_FIRST = 4
+V_FIRST = 2
+FILL_V = 2944
+EDGE = 8
 Q_COL = N
 V_COL = N + NQ
 
@@ -58,7 +60,11 @@ def tile_attend_pkv8q_silu_kernel(
         nc.vector.memset(warm[:, 0:1], 0.0)
         nc.vector.memset(vsc_pool[:].bitcast(I32), 0)
         nc.vector.memset(planes[:, Q_COL:V_COL].bitcast(I32), 0)
-        nc.vector.memset(vs_pool[0:VS_ROW, :].bitcast(I32), 0)
+        late = vs_pool[0:VS_ROW, FILL_V:T]
+        edges = late.bitcast(BF16).rearrange("p (a c) -> p a c", c=2 * EDGE)
+        nc.vector.memset(edges[:, 0 :: (T - FILL_V) // EDGE - 1, :], 0.0)
+        nc.vector.memset(vs_pool[0:VS_ROW, 0:FILL_V].bitcast(I32), 0)
+        nc.gpsimd.memset(late[:, EDGE : T - FILL_V - EDGE].bitcast(I32), 0)
         nc.scalar.activation(warm[:, 1:2], warm[:, 0:1], SILU)
 
         kw_hbm = k_words[0].rearrange("p n t -> p (n t)").bitcast(I32)

from contextlib import ExitStack

import concourse.mybir as mybir

P = 128
T = 4096
N = 1024
PAGE = 512
PAGES = N // PAGE
POOL_PAGES = T // PAGE
NQ = 128
DV = 128
D = 512
PACK = 4
PAIR = 2
HALF = NQ // 2
VS_ROW = P - 1
SPREAD = 8
K_FIRST = 256
V_FIRST = 2
FILL_V = 2944
EDGE = 8
Q_COL = N
V_COL = N + NQ

FLOPS = 2 * NQ * N * D + 2 * NQ * N * DV

F32 = mybir.dt.float32
BF16 = mybir.dt.bfloat16
I32 = mybir.dt.int32
U32 = mybir.dt.uint32
U16 = mybir.dt.uint16
U8 = mybir.dt.uint8
FP8X4 = mybir.dt.float8_e4m3fn_x4
MULT = mybir.AluOpType.mult
SILU = mybir.ActivationFunctionType.Silu
COPY = mybir.ActivationFunctionType.Copy


def tile_attend_pkv8q_silu_kernel(
    tc, q_words, q_scales, k_words, k_scales, v_words, v_scales, vs, offs, voffs, out
):
    nc = tc.nc
    with ExitStack() as ctx:
        sb = ctx.enter_context(tc.tile_pool(name="sb", bufs=1))
        ps = ctx.enter_context(tc.psum_pool(name="ps", bufs=1))

        offs_t = sb.tile([P, N // 16], U16, name="offs_t")
        voffs_t = sb.tile([P, PAGES * DV // 16], U16, name="voffs_t")
        kw_pool = sb.tile([P, T], I32, name="kw_pool", align_bytes=64)
        ks_pool = sb.tile([P, T], U8, name="ks_pool", align_bytes=64)
        vs_pool = sb.tile([P, T], F32, name="vs_pool", align_bytes=64)
        vsc_pool = sb.tile([P, POOL_PAGES * DV], U8, name="vsc_pool", align_bytes=64)
        vw_pool = sb.tile([P, POOL_PAGES * DV], I32, name="vw_pool", align_bytes=64)
        qw = sb.tile([P, NQ], I32, name="qw", align_bytes=64)
        planes = sb.tile([P, V_COL + PAGES * DV], U8, name="planes", align_bytes=64)

        nc.vector.memset(ks_pool[:].bitcast(I32), 0)
        warm = sb.tile([P, 2], F32, name="warm", align_bytes=64)
        nc.vector.memset(warm[:, 0:1], 0.0)
        nc.vector.memset(vsc_pool[:].bitcast(I32), 0)
        nc.vector.memset(planes[:, Q_COL:V_COL].bitcast(I32), 0)
        late = vs_pool[0:VS_ROW, FILL_V:T]
        edges = late.bitcast(BF16).rearrange("p (a c) -> p a c", c=2 * EDGE)
        nc.vector.memset(edges[:, 0 :: (T - FILL_V) // EDGE - 1, :], 0.0)
        nc.vector.memset(vs_pool[0:VS_ROW, 0:FILL_V].bitcast(I32), 0)
        nc.gpsimd.memset(late[:, EDGE : T - FILL_V - EDGE].bitcast(I32), 0)
        nc.scalar.activation(warm[:, 1:2], warm[:, 0:1], SILU)

        kw_hbm = k_words[0].rearrange("p n t -> p (n t)").bitcast(I32)
        nc.sync.dma_start(vs_pool[VS_ROW:P, :], vs[0:1, :])
        nc.sync.dma_start(kw_pool[:, 0:K_FIRST], kw_hbm[:, 0:K_FIRST])
        nc.sync.dma_start(offs_t[:], offs)
        nc.sync.dma_start(voffs_t[:], voffs)
        nc.sync.dma_start(ks_pool[0:P:SPREAD, :].bitcast(I32), k_scales[0].bitcast(I32))
        nc.sync.dma_start(
            vsc_pool[0:P:SPREAD, :].bitcast(I32).rearrange("r (u e) -> r u e", u=POOL_PAGES),
            v_scales.bitcast(I32).rearrange("u r e -> r u e"),
        )
        nc.sync.dma_start(planes[0:P:SPREAD, Q_COL:V_COL].bitcast(I32), q_scales[0, 0].bitcast(I32))
        nc.sync.dma_start(kw_pool[:, K_FIRST:], kw_hbm[:, K_FIRST:])
        nc.sync.dma_start(qw[:], q_words[0, 0].rearrange("p n t -> p (n t)").bitcast(I32))
        vw_sb = vw_pool[:].rearrange("p (u e) -> p u e", u=POOL_PAGES)
        vw_hbm = v_words.rearrange("u p e t -> p u (e t)").bitcast(I32)
        nc.sync.dma_start(vw_sb[:, 0:V_FIRST, :], vw_hbm[:, 0:V_FIRST, :])

        ks_g = sb.tile([P, N], U8, name="ks_g", align_bytes=64)
        vsc_g = sb.tile([P, PAGES * DV], U8, name="vsc_g", tag="vsc_then_vs", align_bytes=64)

        def page_offs(g):
            return offs_t[:, g * (PAGE // 16) : (g + 1) * (PAGE // 16)]

        nc.vector.tensor_copy(ks_g[:], ks_pool[:].indirect(offs_t[:]))
        nc.vector.tensor_copy(vsc_g[:], vsc_pool[:].indirect(voffs_t[:]))
        nc.vector.tensor_copy(
            planes[:, 0:N].rearrange("p (g t s) -> p g t s", g=PAGES, t=PACK),
            ks_g[:].rearrange("p (g s t) -> p g t s", g=PAGES, t=PACK),
        )
        nc.vector.tensor_copy(planes[:, V_COL:].bitcast(I32), vsc_g[:].bitcast(I32))
        for r in range(1, 4):
            nc.sync.dma_start(planes[r:P:32, :].bitcast(I32), planes[SPREAD * r : P : 32, :].bitcast(I32))
        nc.sync.dma_start(vw_sb[:, V_FIRST:, :], vw_hbm[:, V_FIRST:, :])
        vs_g = sb.tile([P, N], F32, name="vs_g", tag="vsc_then_vs", align_bytes=64)
        vs_t = sb.tile([P, PAGES, PACK], F32, name="vs_t", align_bytes=64)
        vs_by_page = vs_g[:].rearrange("p (s g t) -> p g s t", g=PAGES, t=PACK)
        vs_first = sb.tile([P, PAGE], F32, name="vs_first", align_bytes=64)
        nc.scalar.activation(vs_first[:], vs_pool[:].indirect(page_offs(0)), COPY)
        nc.scalar.activation(vs_by_page[:, 0], vs_first[:].rearrange("p (s t) -> p s t", t=PACK), COPY)
        nc.vector.tensor_copy(vs_by_page[:, 1].bitcast(U32), vs_pool[:].bitcast(U32).indirect(page_offs(1)))
        nc.sync.dma_start(
            vs_t[:].rearrange("p g t -> p (g t)"),
            vs_g[VS_ROW:P, :].rearrange("p (s c) -> p s c", c=PAGES * PACK),
        )

        kw_g = sb.tile([P, N], U32, name="kw_g", align_bytes=64)
        score = [
            [ps.tile([P, PAIR, NQ], F32, name=f"score{g}{u}") for u in range(PACK // PAIR)] for g in range(PAGES)
        ]
        for g in range(PAGES):
            nc.vector.tensor_copy(
                kw_g[:, g * PAGE : (g + 1) * PAGE].rearrange("p (t s) -> p s t", t=PACK),
                kw_pool[:].bitcast(U32).indirect(page_offs(g)),
            )
            for t in range(PACK):
                slots = slice(g * PAGE + t * P, g * PAGE + (t + 1) * P)
                nc.tensor.matmul_mx(
                    out=score[g][t // PAIR][:, t % PAIR, :],
                    lhsT=kw_g[:, slots].bitcast(FP8X4),
                    lhsT_scale=planes[:, slots],
                    rhs=qw[:].bitcast(FP8X4),
                    rhs_scale=planes[:, Q_COL:V_COL],
                    start=True,
                    stop=True,
                )

        vw_g = sb.tile([P, PAGES * DV], U32, name="vw_g", align_bytes=64)
        nc.vector.tensor_copy(vw_g[:], vw_pool[:].bitcast(U32).indirect(voffs_t[:]))

        w16 = [sb.tile([P, NQ, PACK], BF16, name=f"w16_{g}", align_bytes=64) for g in range(PAGES)]
        wsc = [sb.tile([P, NQ], U8, name=f"wsc{g}", align_bytes=64) for g in range(PAGES)]
        halves = [slice(0, HALF), slice(HALF, NQ)]

        for g in range(PAGES):
            p32 = sb.tile([P, 2, PACK // PAIR, HALF, PAIR], F32, name=f"p32_{g}", align_bytes=64)
            nc.scalar.activation(
                p32[:, :, 0, :, :], score[g][0][:].rearrange("p t (h q) -> p h q t", h=2), SILU
            )
            for h, cols in enumerate(halves):
                nc.scalar.activation(p32[:, h, 1, :, :], score[g][1][:, :, cols].rearrange("p t q -> p q t"), SILU)
            for h, cols in enumerate(halves):
                nc.vector.tensor_tensor(
                    w16[g][:, cols, :].rearrange("p q (u t) -> p q u t", t=PAIR),
                    p32[:, h].rearrange("p u q t -> p q u t"),
                    vs_t[:, g, :].rearrange("p (u t) -> p u t", t=PAIR).unsqueeze(1).to_broadcast(
                        [P, HALF, PACK // PAIR, PAIR]
                    ),
                    MULT,
                )
        wq = [
            sb.tile([P, NQ], U32, name="wq0", align_bytes=64),
            sb.tile([P, NQ], U32, name="wq1", align_bytes=64),
        ]

        def quantize(g, cols):
            nc.vector.quantize_mx(
                out=wq[g][:, cols].bitcast(FP8X4),
                scales=wsc[g][:, cols],
                in_=w16[g][:, cols, :].rearrange("p q t -> p (q t)"),
            )

        quantize(0, slice(0, NQ))
        for cols in halves:
            quantize(1, cols)

        acc = ps.tile([P, DV], F32, name="acc")
        for g in range(PAGES):
            nc.tensor.matmul_mx(
                out=acc[:],
                lhsT=wq[g][:].bitcast(FP8X4),
                lhsT_scale=wsc[g][:],
                rhs=vw_g[:, g * DV : (g + 1) * DV].bitcast(FP8X4),
                rhs_scale=planes[:, V_COL + g * DV : V_COL + (g + 1) * DV],
                start=(g == 0),
                stop=(g == PAGES - 1),
            )
        y = sb.tile([P, DV], F32, name="y", align_bytes=64)
        nc.scalar.activation(y[:], acc[:], COPY, scale=1.0 / 16.0)
        nc.sync.dma_start(out[0], y[:])
